import numpy as np
import ml_dtypes


def mxq(x, axis, fmt="e4m3"):
    dtype, down = {"e4m3": (ml_dtypes.float8_e4m3fn, 7), "e5m2": (ml_dtypes.float8_e5m2, 14)}[fmt]
    v = np.moveaxis(np.asarray(x, np.float32).astype(ml_dtypes.bfloat16).astype(np.float64), axis, -1)
    blocks = v.reshape(v.shape[:-1] + (-1, 32))
    amax = np.abs(blocks).max(-1, keepdims=True)
    byte = np.maximum(np.where(amax > 0, np.frexp(amax)[1] - 1 + 127, 0) - down, 1)
    scale = np.exp2(byte - 127.0)
    codes = (blocks / scale).astype(np.float32).astype(dtype).astype(np.float64)
    return np.moveaxis((codes * scale).reshape(v.shape), -1, axis)


WIDE = False


def mx_kscale(k):
    if not WIDE:
        return np.ones(k)
    levels = np.array([10, -10, 5, -5, 0])
    if k % 512:
        return np.exp2(np.random.permutation(np.resize(levels, k // 32))).repeat(32)
    a = np.empty((k // 512, 16))
    for p in range(k // 512):
        a[p, :8] = np.random.permutation(np.resize(levels, 8))
        for g in range(8):
            far = levels[np.abs(levels - a[p, g]) >= 10]
            a[p, g + 8] = far[np.random.randint(len(far))]
    return np.exp2(a.ravel()).repeat(32)


def f64(x):
    return np.asarray(x).astype(np.float64)


def striped(idx):
    return np.tile(idx.reshape(-1, 16).T, (8, 1)).astype(np.uint16)


def unstriped(offs):
    return offs[:16].T.reshape(-1).astype(np.int64)


E2M1 = np.array([0.0, 0.5, 1.0, 1.5, 2.0, 3.0, 4.0, 6.0, -0.0, -0.5, -1.0, -1.5, -2.0, -3.0, -4.0, -6.0])


def pack_weight(w, fmt):
    k, n = w.shape
    w = f64(np.asarray(w, np.float32).astype(ml_dtypes.bfloat16)).reshape(k // 32, 32, n)
    amax = np.abs(w).max(1)
    if fmt == "e4m3":
        byte = np.frexp(amax)[1] - 1 + 127 - 7
    else:
        mant, ex = np.frexp(amax / 6.0)
        byte = np.where(mant > 0.5, ex, ex - 1) + 127
    byte = np.clip(np.where(amax > 0, byte, 1), 1, 254)
    scaled = (w * np.exp2(127.0 - byte)[:, None, :]).reshape(k, n).astype(np.float32)
    by_word = np.ascontiguousarray(scaled.reshape(k // 512, 128, 4, n).transpose(0, 1, 3, 2))
    if fmt == "e4m3":
        words = by_word.astype(ml_dtypes.float8_e4m3fn).view(np.uint8)
    else:
        c = by_word.astype(ml_dtypes.float4_e2m1fn).view(np.uint8) & 0xF
        words = (c[..., 0::2] | (c[..., 1::2] << 4)).reshape(k // 512, 128, 2 * n)
    return np.ascontiguousarray(words), np.ascontiguousarray(byte.astype(np.uint8).reshape(k // 512, 16, n))


def unpack_weight(words, scales, fmt):
    g, _, n = scales.shape
    words = np.ascontiguousarray(words).reshape(g, 128, n, -1)
    if fmt == "e4m3":
        vals = words.view(ml_dtypes.float8_e4m3fn).astype(np.float64)
    else:
        nib = np.empty((g, 128, n, 4), np.uint8)
        nib[..., 0::2] = words & 0xF
        nib[..., 1::2] = words >> 4
        vals = E2M1[nib]
    vals = vals * np.repeat(np.exp2(scales.astype(np.float64) - 127.0), 8, axis=1)[..., None]
    return vals.transpose(0, 1, 3, 2).reshape(g * 512, n)


def pack_table4(v):
    words, scales = pack_weight(v, "e2m1")
    g, t = words.shape[0] // 2, v.shape[1]
    words = words.reshape(g, 2, 128, t, 2).transpose(0, 2, 3, 1, 4)
    return np.concatenate([words.reshape(g, -1), scales.reshape(g, -1)], axis=1)


def unpack_table4(tab):
    g, t = tab.shape[0], tab.shape[1] // 544
    words = tab[:, :512 * t].reshape(g, 128, t, 2, 2).transpose(0, 3, 1, 2, 4).reshape(2 * g, 128, 2 * t)
    return unpack_weight(words, tab[:, 512 * t:].reshape(2 * g, 16, t), "e2m1")


def gelu(v):
    return 0.5 * v * (1.0 + np.tanh(np.sqrt(2.0 / np.pi) * (v + 0.044715 * v**3)))


K, M, T, S = 1024, 1024, 4096, 2048


def setup_inputs():
    n = np.random.standard_normal
    s = mx_kscale(K)[:, None]
    return {
        "tab": pack_table4(n((K, T)) * s),
        "w": (n((K, M)) / np.sqrt(K) / s).astype(np.float32),
        "b": (0.3 * n(1024)).astype(np.float32),
        "offs": striped(np.random.permutation(T)[:S]),
    }


def reference(tab, w, b, offs):
    tab_ = unpack_table4(tab)[:, unstriped(offs)]
    w_ = mxq(f64(w), 0, "e4m3")
    y = w_.T @ tab_
    return gelu(y + f64(b)[:, None])

@@ -1,0 +1,190 @@
+from contextlib import ExitStack
+
+import concourse.mybir as mybir
+from concourse.masks import make_identity
+
+K, M, T, S = 1024, 1024, 4096, 2048
+FLOPS = 2 * K * M * S
+
+F32 = mybir.dt.float32
+BF16 = mybir.dt.bfloat16
+I32 = mybir.dt.int32
+U32 = mybir.dt.uint32
+U16 = mybir.dt.uint16
+U8 = mybir.dt.uint8
+E4M3 = mybir.dt.float8_e4m3fn_x4
+E2M1 = mybir.dt.float4_e2m1fn_x4
+GELU = mybir.ActivationFunctionType.Gelu_apprx_tanh
+
+P = 128
+QUAD = 32
+PACK = 4
+PASSES = K // (P * PACK)
+SCALE_ROWS = K // 32
+M_TILES = M // P
+
+N = 512
+RUN = 1024
+PIECE = 256
+CHUNKS = [(0, 256), (256, 256), (512, 512)]
+
+SHIFTS = (QUAD - 4 - SCALE_ROWS // PASSES, QUAD - 4)
+MOVED = (112, 100)
+
+
+def tile_list_tab4_gelu_kernel(tc, tab, w, b, offs, out):
+    nc = tc.nc
+    with ExitStack() as ctx:
+        keep = ctx.enter_context(tc.tile_pool(name="keep", bufs=1))
+        psum = ctx.enter_context(tc.psum_pool(name="psum", bufs=8))
+
+        offsets = keep.tile([P, S // 16], U16, name="offsets")
+        words = keep.tile([P, T], I32, name="words")
+        table_scales = keep.tile([P, T], U8, name="table_scales", align_bytes=64)
+        b_rows = keep.tile([P, P], F32, name="b_rows")
+        b_cols = keep.tile([P, M_TILES], F32, name="b_cols")
+        identity = keep.tile([P, P], F32, name="identity")
+        warm = keep.tile([P, 1], F32, name="warm")
+        scales = [
+            [keep.tile([P, RUN], U8, name=f"scales{r}{h}", align_bytes=64) for h in range(PASSES)]
+            for r in range(S // RUN)
+        ]
+        parted = [keep.tile([P, PASSES, 2 * N], U8, name=f"parted{s}", align_bytes=64) for s in range(S // N)]
+        results = [keep.tile([P, S], F32, name=f"results{m}") for m in range(M_TILES)]
+        raws, grouped, codes, code_scales = {}, {}, {}, {}
+
+        def load_w(k, tag):
+            c0, width = CHUNKS[k]
+            raws[k] = keep.tile([P, PASSES, PACK, width], F32, name=f"raw{k}", tag=tag, align_bytes=64)
+            for a in range(PASSES):
+                rows = w[P * PACK * a : P * PACK * (a + 1), c0 : c0 + width]
+                nc.sync.dma_start(out=raws[k][:, a, :, :], in_=rows.rearrange("(p i) c -> p i c", i=PACK))
+
+        def group(copy, i, a):
+            k = max(j for j in range(len(CHUNKS)) if CHUNKS[j][0] <= PIECE * i)
+            c0 = PIECE * i - CHUNKS[k][0]
+            if i not in grouped:
+                grouped[i] = keep.tile([P, PASSES, PIECE, PACK], BF16, name=f"grouped{i}", tag=f"turn{i}", align_bytes=64)
+            copy(grouped[i][:, a, :, :], raws[k][:, a, :, c0 : c0 + PIECE].rearrange("p i c -> p c i"))
+
+        def quantize(i):
+            codes[i] = keep.tile([P, PASSES, PIECE], U32, name=f"codes{i}", align_bytes=64)
+            code_scales[i] = keep.tile([P, PASSES, PIECE], U8, name=f"code_scales{i}", align_bytes=64)
+            nc.vector.quantize_mx(
+                out=codes[i][:].rearrange("p a c -> p (a c)").bitcast(E4M3),
+                scales=code_scales[i][:].rearrange("p a c -> p (a c)"),
+                in_=grouped[i][:].rearrange("p a c i -> p (a c i)"),
+            )
+
+        def gather_scales(r):
+            picked = keep.tile([P, RUN], U8, name=f"picked{r}", align_bytes=64)
+            cols = slice(r * RUN // 16, (r + 1) * RUN // 16)
+            nc.vector.tensor_copy(picked[:], table_scales[:].indirect(offsets[:, cols]))
+            for h in range(PASSES):
+                nc.sync.dma_start(
+                    out=scales[r][h][0 : MOVED[h], :].bitcast(I32),
+                    in_=picked[SHIFTS[h] : SHIFTS[h] + MOVED[h], :].bitcast(I32),
+                )
+
+        def gather_words(s, tag):
+            picked = keep.tile([P, N], I32, name=f"picked_words{s}", tag=tag, align_bytes=64)
+            cols = slice(s * N // 16, (s + 1) * N // 16)
+            nc.vector.tensor_copy(picked[:].bitcast(U32), words[:].bitcast(U32).indirect(offsets[:, cols]))
+            halves = parted[s][:].rearrange("p h c -> p (h c)").bitcast(U16)
+            nc.vector.tensor_copy(
+                halves.rearrange("p (h n) -> p h n", h=PASSES),
+                picked[:].bitcast(U16).rearrange("p (n h) -> p h n", h=PASSES),
+            )
+
+        def product(m, s, step=N):
+            acc = psum.tile([P, N], F32, name="acc", tag="acc")
+            piece, m0 = divmod(P * m, PIECE)
+            r, j0 = divmod(N * s, RUN)
+            for a in range(PASSES):
+                nc.tensor.matmul_mx(
+                    out=acc[:],
+                    lhsT=codes[piece][:, a, m0 : m0 + P].bitcast(E4M3),
+                    lhsT_scale=code_scales[piece][:, a, m0 : m0 + P],
+                    rhs=parted[s][:, a, :].bitcast(E2M1),
+                    rhs_scale=scales[r][a][:, j0 : j0 + N],
+                    start=(a == 0),
+                    stop=(a == PASSES - 1),
+                )
+            for c in range(0, N, step):
+                nc.scalar.activation(
+                    results[m][:, N * s + c : N * s + c + step], acc[:, c : c + step], GELU, bias=b_cols[:, m : m + 1]
+                )
+
+        def store(m, c0, c1):
+            nc.sync.dma_start(out=out[P * m : P * m + P, c0:c1], in_=results[m][:, c0:c1])
+
+        nc.sync.dma_start(offsets[:], offs)
+        for q in range(P // QUAD):
+            row0 = 4 * q - SHIFTS[0]
+            start = 512 * T + T * row0
+            nc.sync.dma_start(
+                out=table_scales[QUAD * q : QUAD * (q + 1), :].bitcast(I32),
+                in_=tab[0, start : start + QUAD * T].rearrange("(r t) -> r t", t=T).bitcast(I32),
+            )
+        load_w(0, "raw")
+        nc.sync.dma_start(out=words[:], in_=tab[0, 0 : 512 * T].rearrange("(p c) -> p c", p=P).bitcast(I32))
+
+        nc.vector.memset(warm[:], 0.0)
+        nc.scalar.activation(warm[:], warm[:], GELU)
+        nc.gpsimd.memset(b_rows[:], 0.0)
+        nc.scalar.dma_start(out=b_rows[0:M_TILES, :], in_=b.rearrange("(m p) -> m p", p=P))
+        make_identity(nc, identity[:])
+        for r in range(S // RUN):
+            for h in range(PASSES):
+                nc.gpsimd.memset(scales[r][h][:].bitcast(I32), 0)
+
+        for a in range(PASSES):
+            group(nc.scalar.copy, 0, a)
+        b_bank = psum.tile([P, N], F32, name="b_bank", tag="acc")
+        nc.tensor.transpose(b_bank[:, 0:P], b_rows[:], identity[:])
+        nc.scalar.copy(b_cols[:], b_bank[:, 0:M_TILES])
+
+        gather_scales(0)
+        load_w(1, "raw")
+        quantize(0)
+        gather_scales(1)
+        load_w(2, "turn0")
+        gather_words(0, "words01")
+        group(nc.scalar.copy, 1, 0)
+        for m in (0, 1):
+            product(m, 0)
+            store(m, 0, N)
+        gather_words(1, "words01")
+        for m in (0, 1):
+            product(m, 1)
+            store(m, N, 2 * N)
+        group(nc.vector.tensor_copy, 1, 1)
+        quantize(1)
+        for m in (2, 3):
+            product(m, 0)
+            product(m, 1)
+            store(m, 0, 2 * N)
+        gather_words(2, "turn1")
+        for m in range(4):
+            product(m, 2)
+        gather_words(3, "turn1")
+        for m in range(4):
+            product(m, 3)
+            store(m, 2 * N, 4 * N)
+        for i in (2, 3):
+            for a in range(PASSES):
+                group(nc.vector.tensor_copy, i, a)
+            quantize(i)
+        for m in range(4, M_TILES):
+            product(m, 0)
+            product(m, 1)
+            store(m, 0, 2 * N)
+            product(m, 2)
+            if m < M_TILES - 1:
+                product(m, 3)
+                store(m, 2 * N, 4 * N)
+        m, half = M_TILES - 1, N // 2
+        store(m, 2 * N, 3 * N)
+        product(m, 3, step=half)
+        store(m, 3 * N, 3 * N + half)
+        store(m, 3 * N + half, 4 * N)

@@ -24,8 +24,7 @@ SCALE_ROWS = K // 32
 M_TILES = M // P
 
 N = 512
-RUN = 1024
-PIECE = 256
+SLICES = S // N
 CHUNKS = [(0, 256), (256, 256), (512, 512)]
 
 SHIFTS = (QUAD - 4 - SCALE_ROWS // PASSES, QUAD - 4)
@@ -45,78 +44,65 @@ def tile_list_tab4_gelu_kernel(tc, tab, w, b, offs, out):
         b_cols = keep.tile([P, M_TILES], F32, name="b_cols")
         identity = keep.tile([P, P], F32, name="identity")
         warm = keep.tile([P, 1], F32, name="warm")
-        scales = [
-            [keep.tile([P, RUN], U8, name=f"scales{r}{h}", align_bytes=64) for h in range(PASSES)]
-            for r in range(S // RUN)
-        ]
-        parted = [keep.tile([P, PASSES, 2 * N], U8, name=f"parted{s}", align_bytes=64) for s in range(S // N)]
+        scales = [keep.tile([P, S], U8, name=f"scales{h}", align_bytes=64) for h in range(PASSES)]
+        parted = [keep.tile([P, PASSES, 2 * N], U8, name=f"parted{s}", align_bytes=64) for s in range(SLICES)]
         results = [keep.tile([P, S], F32, name=f"results{m}") for m in range(M_TILES)]
         raws, grouped, codes, code_scales = {}, {}, {}, {}
 
         def load_w(k, tag):
             c0, width = CHUNKS[k]
-            raws[k] = keep.tile([P, PASSES, PACK, width], F32, name=f"raw{k}", tag=tag, align_bytes=64)
+            raw = keep.tile([P, PASSES * PACK * width], F32, name=f"raw{k}", tag=tag, align_bytes=64)
             for a in range(PASSES):
+                raws[k, a] = raw[:, a * PACK * width : (a + 1) * PACK * width].rearrange("p (i c) -> p i c", i=PACK)
                 rows = w[P * PACK * a : P * PACK * (a + 1), c0 : c0 + width]
-                nc.sync.dma_start(out=raws[k][:, a, :, :], in_=rows.rearrange("(p i) c -> p i c", i=PACK))
+                nc.sync.dma_start(out=raws[k, a], in_=rows.rearrange("(p i) c -> p i c", i=PACK))
 
-        def group(copy, i, a):
-            k = max(j for j in range(len(CHUNKS)) if CHUNKS[j][0] <= PIECE * i)
-            c0 = PIECE * i - CHUNKS[k][0]
-            if i not in grouped:
-                grouped[i] = keep.tile([P, PASSES, PIECE, PACK], BF16, name=f"grouped{i}", tag=f"turn{i}", align_bytes=64)
-            copy(grouped[i][:, a, :, :], raws[k][:, a, :, c0 : c0 + PIECE].rearrange("p i c -> p c i"))
+        def pair_tile(i, tag):
+            grouped[i] = keep.tile([P, 2, PASSES, P, PACK], BF16, name=f"grouped{i}", tag=tag, align_bytes=64)
 
-        def quantize(i):
-            codes[i] = keep.tile([P, PASSES, PIECE], U32, name=f"codes{i}", align_bytes=64)
-            code_scales[i] = keep.tile([P, PASSES, PIECE], U8, name=f"code_scales{i}", align_bytes=64)
+        def group(copy, m, a):
+            k = max(j for j in range(len(CHUNKS)) if CHUNKS[j][0] <= P * m)
+            c0 = P * m - CHUNKS[k][0]
+            copy(grouped[m // 2][:, m % 2, a, :, :], raws[k, a][:, :, c0 : c0 + P].rearrange("p i c -> p c i"))
+
+        def quantize(m):
+            codes[m] = keep.tile([P, PASSES, P], U32, name=f"codes{m}", align_bytes=64)
+            code_scales[m] = keep.tile([P, PASSES, P], U8, name=f"code_scales{m}", align_bytes=64)
             nc.vector.quantize_mx(
-                out=codes[i][:].rearrange("p a c -> p (a c)").bitcast(E4M3),
-                scales=code_scales[i][:].rearrange("p a c -> p (a c)"),
-                in_=grouped[i][:].rearrange("p a c i -> p (a c i)"),
+                out=codes[m][:].rearrange("p a c -> p (a c)").bitcast(E4M3),
+                scales=code_scales[m][:].rearrange("p a c -> p (a c)"),
+                in_=grouped[m // 2][:, m % 2].rearrange("p a c i -> p (a c i)"),
             )
 
-        def gather_scales(r):
-            picked = keep.tile([P, RUN], U8, name=f"picked{r}", align_bytes=64)
-            cols = slice(r * RUN // 16, (r + 1) * RUN // 16)
-            nc.vector.tensor_copy(picked[:], table_scales[:].indirect(offsets[:, cols]))
-            for h in range(PASSES):
-                nc.sync.dma_start(
-                    out=scales[r][h][0 : MOVED[h], :].bitcast(I32),
-                    in_=picked[SHIFTS[h] : SHIFTS[h] + MOVED[h], :].bitcast(I32),
+        def gather_words(pair, tag):
+            picked = keep.tile([P, 2, N], I32, name=f"picked_words{pair}", tag=tag, align_bytes=64)
+            for j in range(2):
+                s = 2 * pair + j
+                cols = slice(s * N // 16, (s + 1) * N // 16)
+                nc.vector.tensor_copy(picked[:, j, :].bitcast(U32), words[:].bitcast(U32).indirect(offsets[:, cols]))
+            for j in range(2):
+                halves = parted[2 * pair + j][:].rearrange("p h c -> p (h c)").bitcast(U16)
+                nc.vector.tensor_copy(
+                    halves.rearrange("p (h n) -> p h n", h=PASSES),
+                    picked[:, j, :].bitcast(U16).rearrange("p (n h) -> p h n", h=PASSES),
                 )
 
-        def gather_words(s, tag):
-            picked = keep.tile([P, N], I32, name=f"picked_words{s}", tag=tag, align_bytes=64)
-            cols = slice(s * N // 16, (s + 1) * N // 16)
-            nc.vector.tensor_copy(picked[:].bitcast(U32), words[:].bitcast(U32).indirect(offsets[:, cols]))
-            halves = parted[s][:].rearrange("p h c -> p (h c)").bitcast(U16)
-            nc.vector.tensor_copy(
-                halves.rearrange("p (h n) -> p h n", h=PASSES),
-                picked[:].bitcast(U16).rearrange("p (n h) -> p h n", h=PASSES),
-            )
-
-        def product(m, s, step=N):
+        def product(m, s):
             acc = psum.tile([P, N], F32, name="acc", tag="acc")
-            piece, m0 = divmod(P * m, PIECE)
-            r, j0 = divmod(N * s, RUN)
             for a in range(PASSES):
                 nc.tensor.matmul_mx(
                     out=acc[:],
-                    lhsT=codes[piece][:, a, m0 : m0 + P].bitcast(E4M3),
-                    lhsT_scale=code_scales[piece][:, a, m0 : m0 + P],
+                    lhsT=codes[m][:, a, :].bitcast(E4M3),
+                    lhsT_scale=code_scales[m][:, a, :],
                     rhs=parted[s][:, a, :].bitcast(E2M1),
-                    rhs_scale=scales[r][a][:, j0 : j0 + N],
+                    rhs_scale=scales[a][:, N * s : N * (s + 1)],
                     start=(a == 0),
                     stop=(a == PASSES - 1),
                 )
-            for c in range(0, N, step):
-                nc.scalar.activation(
-                    results[m][:, N * s + c : N * s + c + step], acc[:, c : c + step], GELU, bias=b_cols[:, m : m + 1]
-                )
+            nc.scalar.activation(results[m][:, N * s : N * (s + 1)], acc[:], GELU, bias=b_cols[:, m : m + 1])
 
-        def store(m, c0, c1):
-            nc.sync.dma_start(out=out[P * m : P * m + P, c0:c1], in_=results[m][:, c0:c1])
+        def store(m):
+            nc.sync.dma_start(out=out[P * m : P * m + P, :], in_=results[m][:])
 
         nc.sync.dma_start(offsets[:], offs)
         for q in range(P // QUAD):
@@ -126,65 +112,51 @@ def tile_list_tab4_gelu_kernel(tc, tab, w, b, offs, out):
                 out=table_scales[QUAD * q : QUAD * (q + 1), :].bitcast(I32),
                 in_=tab[0, start : start + QUAD * T].rearrange("(r t) -> r t", t=T).bitcast(I32),
             )
-        load_w(0, "raw")
         nc.sync.dma_start(out=words[:], in_=tab[0, 0 : 512 * T].rearrange("(p c) -> p c", p=P).bitcast(I32))
+        for k in range(len(CHUNKS) - 1):
+            load_w(k, f"raw{k}")
 
         nc.vector.memset(warm[:], 0.0)
         nc.scalar.activation(warm[:], warm[:], GELU)
         nc.gpsimd.memset(b_rows[:], 0.0)
         nc.scalar.dma_start(out=b_rows[0:M_TILES, :], in_=b.rearrange("(m p) -> m p", p=P))
         make_identity(nc, identity[:])
-        for r in range(S // RUN):
-            for h in range(PASSES):
-                nc.gpsimd.memset(scales[r][h][:].bitcast(I32), 0)
-
-        for a in range(PASSES):
-            group(nc.scalar.copy, 0, a)
+        for h in range(PASSES):
+            nc.vector.memset(scales[h][:].bitcast(I32), 0)
         b_bank = psum.tile([P, N], F32, name="b_bank", tag="acc")
         nc.tensor.transpose(b_bank[:, 0:P], b_rows[:], identity[:])
         nc.scalar.copy(b_cols[:], b_bank[:, 0:M_TILES])
 
-        gather_scales(0)
-        load_w(1, "raw")
-        quantize(0)
-        gather_scales(1)
-        load_w(2, "turn0")
-        gather_words(0, "words01")
-        group(nc.scalar.copy, 1, 0)
+        picked_scales = keep.tile([P, S], U8, name="picked_scales", tag="late", align_bytes=64)
+        nc.vector.tensor_copy(picked_scales[:], table_scales[:].indirect(offsets[:]))
+        for h in range(PASSES):
+            nc.scalar.dma_start(
+                out=scales[h][0 : MOVED[h], :].bitcast(I32),
+                in_=picked_scales[SHIFTS[h] : SHIFTS[h] + MOVED[h], :].bitcast(I32),
+            )
+
+        load_w(len(CHUNKS) - 1, "late")
+        gather_words(0, "first")
+        pair_tile(0, "turn")
+        for a in range(PASSES):
+            for m in (0, 1):
+                group(nc.scalar.copy, m, a)
         for m in (0, 1):
-            product(m, 0)
-            store(m, 0, N)
-        gather_words(1, "words01")
+            quantize(m)
+        gather_words(1, "turn")
+        for s in range(SLICES):
+            for m in (0, 1):
+                product(m, s)
         for m in (0, 1):
-            product(m, 1)
-            store(m, N, 2 * N)
-        group(nc.vector.tensor_copy, 1, 1)
-        quantize(1)
-        for m in (2, 3):
-            product(m, 0)
-            product(m, 1)
-            store(m, 0, 2 * N)
-        gather_words(2, "turn1")
-        for m in range(4):
-            product(m, 2)
-        gather_words(3, "turn1")
-        for m in range(4):
-            product(m, 3)
-            store(m, 2 * N, 4 * N)
-        for i in (2, 3):
-            for a in range(PASSES):
-                group(nc.vector.tensor_copy, i, a)
-            quantize(i)
-        for m in range(4, M_TILES):
-            product(m, 0)
-            product(m, 1)
-            store(m, 0, 2 * N)
-            product(m, 2)
-            if m < M_TILES - 1:
-                product(m, 3)
-                store(m, 2 * N, 4 * N)
-        m, half = M_TILES - 1, N // 2
-        store(m, 2 * N, 3 * N)
-        product(m, 3, step=half)
-        store(m, 3 * N, 3 * N + half)
-        store(m, 3 * N + half, 4 * N)
+            store(m)
+        for i in range(1, M_TILES // 2):
+            pair_tile(i, "turn" if i == 1 else f"later{i}")
+            for m in (2 * i, 2 * i + 1):
+                for a in range(PASSES):
+                    group(nc.vector.tensor_copy, m, a)
+            for m in (2 * i, 2 * i + 1):
+                quantize(m)
+        for m in range(2, M_TILES):
+            for s in range(SLICES):
+                product(m, s)
+            store(m)

@@ -25,6 +25,8 @@ M_TILES = M // P
 
 N = 512
 SLICES = S // N
+TURN = (0, 1, 1, 0, 1, 0, 1, 0)
+RUN = 1024
 CHUNKS = [(0, 256), (256, 256), (512, 512)]
 
 SHIFTS = (QUAD - 4 - SCALE_ROWS // PASSES, QUAD - 4)
@@ -39,31 +41,37 @@ def tile_list_tab4_gelu_kernel(tc, tab, w, b, offs, out):
 
         offsets = keep.tile([P, S // 16], U16, name="offsets")
         words = keep.tile([P, T], I32, name="words")
-        table_scales = keep.tile([P, T], U8, name="table_scales", align_bytes=64)
+        table_scales = keep.tile([P, T], U8, name="table_scales", tag="late", align_bytes=64)
         b_rows = keep.tile([P, P], F32, name="b_rows")
         b_cols = keep.tile([P, M_TILES], F32, name="b_cols")
         identity = keep.tile([P, P], F32, name="identity")
         warm = keep.tile([P, 1], F32, name="warm")
-        scales = [keep.tile([P, S], U8, name=f"scales{h}", align_bytes=64) for h in range(PASSES)]
+        scales = [
+            [keep.tile([P, RUN], U8, name=f"scales{r}{h}", align_bytes=64) for h in range(PASSES)]
+            for r in range(S // RUN)
+        ]
         parted = [keep.tile([P, PASSES, 2 * N], U8, name=f"parted{s}", align_bytes=64) for s in range(SLICES)]
         results = [keep.tile([P, S], F32, name=f"results{m}") for m in range(M_TILES)]
-        raws, grouped, codes, code_scales = {}, {}, {}, {}
+        raws, grouped, codes, code_scales, picked = {}, {}, {}, {}, {}
 
-        def load_w(k, tag):
-            c0, width = CHUNKS[k]
-            raw = keep.tile([P, PASSES * PACK * width], F32, name=f"raw{k}", tag=tag, align_bytes=64)
-            for a in range(PASSES):
-                raws[k, a] = raw[:, a * PACK * width : (a + 1) * PACK * width].rearrange("p (i c) -> p i c", i=PACK)
-                rows = w[P * PACK * a : P * PACK * (a + 1), c0 : c0 + width]
-                nc.sync.dma_start(out=raws[k, a], in_=rows.rearrange("(p i) c -> p i c", i=PACK))
-
-        def pair_tile(i, tag):
-            grouped[i] = keep.tile([P, 2, PASSES, P, PACK], BF16, name=f"grouped{i}", tag=tag, align_bytes=64)
+        def load_w(chunks, tag):
+            total = sum(CHUNKS[k][1] for k in chunks)
+            raw = keep.tile([P, PASSES * PACK * total], F32, name=f"raw{chunks[0]}", tag=tag, align_bytes=64)
+            at = 0
+            for k in chunks:
+                c0, width = CHUNKS[k]
+                for a in range(PASSES):
+                    raws[k, a] = raw[:, at : at + PACK * width].rearrange("p (i c) -> p i c", i=PACK)
+                    at = at + PACK * width
+                    rows = w[P * PACK * a : P * PACK * (a + 1), c0 : c0 + width]
+                    nc.sync.dma_start(out=raws[k, a], in_=rows.rearrange("(p i) c -> p i c", i=PACK))
 
         def group(copy, m, a):
             k = max(j for j in range(len(CHUNKS)) if CHUNKS[j][0] <= P * m)
             c0 = P * m - CHUNKS[k][0]
-            copy(grouped[m // 2][:, m % 2, a, :, :], raws[k, a][:, :, c0 : c0 + P].rearrange("p i c -> p c i"))
+            if m not in grouped:
+                grouped[m] = keep.tile([P, PASSES, P, PACK], BF16, name=f"grouped{m}", tag=f"turn{TURN[m]}", align_bytes=64)
+            copy(grouped[m][:, a, :, :], raws[k, a][:, :, c0 : c0 + P].rearrange("p i c -> p c i"))
 
         def quantize(m):
             codes[m] = keep.tile([P, PASSES, P], U32, name=f"codes{m}", align_bytes=64)
@@ -71,38 +79,46 @@ def tile_list_tab4_gelu_kernel(tc, tab, w, b, offs, out):
             nc.vector.quantize_mx(
                 out=codes[m][:].rearrange("p a c -> p (a c)").bitcast(E4M3),
                 scales=code_scales[m][:].rearrange("p a c -> p (a c)"),
-                in_=grouped[m // 2][:, m % 2].rearrange("p a c i -> p (a c i)"),
+                in_=grouped[m][:].rearrange("p a c i -> p (a c i)"),
             )
 
-        def gather_words(pair, tag):
-            picked = keep.tile([P, 2, N], I32, name=f"picked_words{pair}", tag=tag, align_bytes=64)
-            for j in range(2):
-                s = 2 * pair + j
-                cols = slice(s * N // 16, (s + 1) * N // 16)
-                nc.vector.tensor_copy(picked[:, j, :].bitcast(U32), words[:].bitcast(U32).indirect(offsets[:, cols]))
-            for j in range(2):
-                halves = parted[2 * pair + j][:].rearrange("p h c -> p (h c)").bitcast(U16)
-                nc.vector.tensor_copy(
-                    halves.rearrange("p (h n) -> p h n", h=PASSES),
-                    picked[:, j, :].bitcast(U16).rearrange("p (n h) -> p h n", h=PASSES),
-                )
+        def gather_words(s, tag):
+            picked[s] = keep.tile([P, N], I32, name=f"picked_words{s}", tag=tag, align_bytes=64)
+            cols = slice(s * N // 16, (s + 1) * N // 16)
+            nc.vector.tensor_copy(picked[s][:].bitcast(U32), words[:].bitcast(U32).indirect(offsets[:, cols]))
 
-        def product(m, s):
+        def part(s):
+            halves = parted[s][:].rearrange("p h c -> p (h c)").bitcast(U16)
+            nc.vector.tensor_copy(
+                halves.rearrange("p (h n) -> p h n", h=PASSES),
+                picked[s][:].bitcast(U16).rearrange("p (n h) -> p h n", h=PASSES),
+            )
+
+        def prepare(m):
+            for a in range(PASSES):
+                group(nc.vector.tensor_copy, m, a)
+            quantize(m)
+
+        def product(m, s, step=N):
             acc = psum.tile([P, N], F32, name="acc", tag="acc")
+            r, j0 = divmod(N * s, RUN)
             for a in range(PASSES):
                 nc.tensor.matmul_mx(
                     out=acc[:],
                     lhsT=codes[m][:, a, :].bitcast(E4M3),
                     lhsT_scale=code_scales[m][:, a, :],
                     rhs=parted[s][:, a, :].bitcast(E2M1),
-                    rhs_scale=scales[a][:, N * s : N * (s + 1)],
+                    rhs_scale=scales[r][a][:, j0 : j0 + N],
                     start=(a == 0),
                     stop=(a == PASSES - 1),
                 )
-            nc.scalar.activation(results[m][:, N * s : N * (s + 1)], acc[:], GELU, bias=b_cols[:, m : m + 1])
+            for c in range(0, N, step):
+                nc.scalar.activation(
+                    results[m][:, N * s + c : N * s + c + step], acc[:, c : c + step], GELU, bias=b_cols[:, m : m + 1]
+                )
 
-        def store(m):
-            nc.sync.dma_start(out=out[P * m : P * m + P, :], in_=results[m][:])
+        def store(m, c0, c1):
+            nc.sync.dma_start(out=out[P * m : P * m + P, c0:c1], in_=results[m][:, c0:c1])
 
         nc.sync.dma_start(offsets[:], offs)
         for q in range(P // QUAD):
@@ -113,50 +129,68 @@ def tile_list_tab4_gelu_kernel(tc, tab, w, b, offs, out):
                 in_=tab[0, start : start + QUAD * T].rearrange("(r t) -> r t", t=T).bitcast(I32),
             )
         nc.sync.dma_start(out=words[:], in_=tab[0, 0 : 512 * T].rearrange("(p c) -> p c", p=P).bitcast(I32))
-        for k in range(len(CHUNKS) - 1):
-            load_w(k, f"raw{k}")
+        load_w([0], "early")
 
         nc.vector.memset(warm[:], 0.0)
         nc.scalar.activation(warm[:], warm[:], GELU)
         nc.gpsimd.memset(b_rows[:], 0.0)
         nc.scalar.dma_start(out=b_rows[0:M_TILES, :], in_=b.rearrange("(m p) -> m p", p=P))
         make_identity(nc, identity[:])
-        for h in range(PASSES):
-            nc.vector.memset(scales[h][:].bitcast(I32), 0)
+        for r in range(S // RUN):
+            for h in range(PASSES):
+                nc.vector.memset(scales[r][h][:].bitcast(I32), 0)
         b_bank = psum.tile([P, N], F32, name="b_bank", tag="acc")
         nc.tensor.transpose(b_bank[:, 0:P], b_rows[:], identity[:])
         nc.scalar.copy(b_cols[:], b_bank[:, 0:M_TILES])
 
-        picked_scales = keep.tile([P, S], U8, name="picked_scales", tag="late", align_bytes=64)
-        nc.vector.tensor_copy(picked_scales[:], table_scales[:].indirect(offsets[:]))
-        for h in range(PASSES):
-            nc.scalar.dma_start(
-                out=scales[h][0 : MOVED[h], :].bitcast(I32),
-                in_=picked_scales[SHIFTS[h] : SHIFTS[h] + MOVED[h], :].bitcast(I32),
-            )
+        for r in range(S // RUN):
+            picked_scales = keep.tile([P, RUN], U8, name=f"picked_scales{r}", align_bytes=64)
+            cols = slice(r * RUN // 16, (r + 1) * RUN // 16)
+            nc.vector.tensor_copy(picked_scales[:], table_scales[:].indirect(offsets[:, cols]))
+            for h in range(PASSES):
+                nc.sync.dma_start(
+                    out=scales[r][h][0 : MOVED[h], :].bitcast(I32),
+                    in_=picked_scales[SHIFTS[h] : SHIFTS[h] + MOVED[h], :].bitcast(I32),
+                )
 
-        load_w(len(CHUNKS) - 1, "late")
-        gather_words(0, "first")
-        pair_tile(0, "turn")
+        load_w([1, 2], "late")
+        for s in (0, 1):
+            gather_words(s, f"first{s}")
+            part(s)
         for a in range(PASSES):
             for m in (0, 1):
                 group(nc.scalar.copy, m, a)
         for m in (0, 1):
             quantize(m)
-        gather_words(1, "turn")
-        for s in range(SLICES):
-            for m in (0, 1):
-                product(m, s)
         for m in (0, 1):
-            store(m)
-        for i in range(1, M_TILES // 2):
-            pair_tile(i, "turn" if i == 1 else f"later{i}")
-            for m in (2 * i, 2 * i + 1):
-                for a in range(PASSES):
-                    group(nc.vector.tensor_copy, m, a)
-            for m in (2 * i, 2 * i + 1):
-                quantize(m)
-        for m in range(2, M_TILES):
+            product(m, 0)
+            product(m, 1)
+            store(m, 0, 2 * N)
+        gather_words(2, "turn0")
+        part(2)
+        prepare(2)
+        for m in (0, 1):
+            product(m, 2)
+        for s in range(3):
+            product(2, s)
+        store(2, 0, 2 * N)
+        gather_words(3, "turn1")
+        part(3)
+        for m in range(3):
+            product(m, 3)
+            store(m, 2 * N, 4 * N)
+        for m in range(3, M_TILES):
+            prepare(m)
+        for m in range(3, M_TILES - 1):
             for s in range(SLICES):
                 product(m, s)
-            store(m)
+            store(m, 0, S)
+        m, half = M_TILES - 1, N // 2
+        product(m, 0)
+        product(m, 1)
+        store(m, 0, 2 * N)
+        product(m, 2)
+        store(m, 2 * N, 3 * N)
+        product(m, 3, step=half)
+        store(m, 3 * N, 3 * N + half)
+        store(m, 3 * N + half, S)

@@ -25,7 +25,6 @@ M_TILES = M // P
 
 N = 512
 SLICES = S // N
-TURN = (0, 1, 1, 0, 1, 0, 1, 0)
 RUN = 1024
 CHUNKS = [(0, 256), (256, 256), (512, 512)]
 
@@ -50,36 +49,55 @@ def tile_list_tab4_gelu_kernel(tc, tab, w, b, offs, out):
             [keep.tile([P, RUN], U8, name=f"scales{r}{h}", align_bytes=64) for h in range(PASSES)]
             for r in range(S // RUN)
         ]
-        parted = [keep.tile([P, PASSES, 2 * N], U8, name=f"parted{s}", align_bytes=64) for s in range(SLICES)]
         results = [keep.tile([P, S], F32, name=f"results{m}") for m in range(M_TILES)]
-        raws, grouped, codes, code_scales, picked = {}, {}, {}, {}, {}
+        raws, grouped, codes, code_scales, picked, parted, picked_scales = {}, {}, {}, {}, {}, {}, {}
 
-        def load_w(chunks, tag):
-            total = sum(CHUNKS[k][1] for k in chunks)
-            raw = keep.tile([P, PASSES * PACK * total], F32, name=f"raw{chunks[0]}", tag=tag, align_bytes=64)
+        def raw_tile(pieces, tag):
+            total = sum(CHUNKS[k][1] for k, a in pieces)
+            raw = keep.tile([P, PACK * total], F32, name=f"raw_{tag}", tag=tag, align_bytes=64)
             at = 0
-            for k in chunks:
-                c0, width = CHUNKS[k]
-                for a in range(PASSES):
-                    raws[k, a] = raw[:, at : at + PACK * width].rearrange("p (i c) -> p i c", i=PACK)
-                    at = at + PACK * width
-                    rows = w[P * PACK * a : P * PACK * (a + 1), c0 : c0 + width]
-                    nc.sync.dma_start(out=raws[k, a], in_=rows.rearrange("(p i) c -> p i c", i=PACK))
+            for k, a in pieces:
+                raws[k, a] = raw[:, at : at + PACK * CHUNKS[k][1]].rearrange("p (i c) -> p i c", i=PACK)
+                at = at + PACK * CHUNKS[k][1]
+
+        def load_w(k, a):
+            c0, width = CHUNKS[k]
+            rows = w[P * PACK * a : P * PACK * (a + 1), c0 : c0 + width]
+            nc.sync.dma_start(out=raws[k, a], in_=rows.rearrange("(p i) c -> p i c", i=PACK))
+
+        def gather_scales(r):
+            picked_scales[r] = keep.tile([P, RUN], U8, name=f"picked_scales{r}", align_bytes=64)
+            cols = slice(r * RUN // 16, (r + 1) * RUN // 16)
+            nc.vector.tensor_copy(picked_scales[r][:], table_scales[:].indirect(offsets[:, cols]))
+
+        def move_scales(r, queue):
+            for h in range(PASSES):
+                queue.dma_start(
+                    out=scales[r][h][0 : MOVED[h], :].bitcast(I32),
+                    in_=picked_scales[r][SHIFTS[h] : SHIFTS[h] + MOVED[h], :].bitcast(I32),
+                )
+
+        def group_tile(tiles, tag):
+            shared = keep.tile([P, len(tiles), PASSES, P, PACK], BF16, name=f"grouped{tiles[0]}", tag=tag, align_bytes=64)
+            for j, m in enumerate(tiles):
+                grouped[m] = shared[:, j]
 
         def group(copy, m, a):
             k = max(j for j in range(len(CHUNKS)) if CHUNKS[j][0] <= P * m)
             c0 = P * m - CHUNKS[k][0]
-            if m not in grouped:
-                grouped[m] = keep.tile([P, PASSES, P, PACK], BF16, name=f"grouped{m}", tag=f"turn{TURN[m]}", align_bytes=64)
-            copy(grouped[m][:, a, :, :], raws[k, a][:, :, c0 : c0 + P].rearrange("p i c -> p c i"))
+            copy(
+                grouped[m][:, a, :, :].rearrange("p (c j) i -> p c i j", j=PACK),
+                raws[k, a][:, :, c0 : c0 + P].rearrange("p i (c j) -> p c i j", j=PACK),
+            )
 
-        def quantize(m):
-            codes[m] = keep.tile([P, PASSES, P], U32, name=f"codes{m}", align_bytes=64)
-            code_scales[m] = keep.tile([P, PASSES, P], U8, name=f"code_scales{m}", align_bytes=64)
+        def quantize(m, a0=0, a1=PASSES):
+            if m not in codes:
+                codes[m] = keep.tile([P, PASSES, P], U32, name=f"codes{m}", align_bytes=64)
+                code_scales[m] = keep.tile([P, PASSES, P], U8, name=f"code_scales{m}", align_bytes=64)
             nc.vector.quantize_mx(
-                out=codes[m][:].rearrange("p a c -> p (a c)").bitcast(E4M3),
-                scales=code_scales[m][:].rearrange("p a c -> p (a c)"),
-                in_=grouped[m][:].rearrange("p a c i -> p (a c i)"),
+                out=codes[m][:, a0:a1, :].rearrange("p a c -> p (a c)").bitcast(E4M3),
+                scales=code_scales[m][:, a0:a1, :].rearrange("p a c -> p (a c)"),
+                in_=grouped[m][:, a0:a1].rearrange("p a c i -> p (a c i)"),
             )
 
         def gather_words(s, tag):
@@ -87,7 +105,8 @@ def tile_list_tab4_gelu_kernel(tc, tab, w, b, offs, out):
             cols = slice(s * N // 16, (s + 1) * N // 16)
             nc.vector.tensor_copy(picked[s][:].bitcast(U32), words[:].bitcast(U32).indirect(offsets[:, cols]))
 
-        def part(s):
+        def part(s, tag):
+            parted[s] = keep.tile([P, PASSES, 2 * N], U8, name=f"parted{s}", tag=tag, align_bytes=64)
             halves = parted[s][:].rearrange("p h c -> p (h c)").bitcast(U16)
             nc.vector.tensor_copy(
                 halves.rearrange("p (h n) -> p h n", h=PASSES),
@@ -99,26 +118,25 @@ def tile_list_tab4_gelu_kernel(tc, tab, w, b, offs, out):
                 group(nc.vector.tensor_copy, m, a)
             quantize(m)
 
-        def product(m, s, step=N):
-            acc = psum.tile([P, N], F32, name="acc", tag="acc")
-            r, j0 = divmod(N * s, RUN)
+        def product(m, s, c0=0, width=N):
+            acc = psum.tile([P, width], F32, name="acc", tag="acc")
+            r, j0 = divmod(N * s + c0, RUN)
             for a in range(PASSES):
                 nc.tensor.matmul_mx(
                     out=acc[:],
                     lhsT=codes[m][:, a, :].bitcast(E4M3),
                     lhsT_scale=code_scales[m][:, a, :],
-                    rhs=parted[s][:, a, :].bitcast(E2M1),
-                    rhs_scale=scales[r][a][:, j0 : j0 + N],
+                    rhs=parted[s][:, a, 2 * c0 : 2 * (c0 + width)].bitcast(E2M1),
+                    rhs_scale=scales[r][a][:, j0 : j0 + width],
                     start=(a == 0),
                     stop=(a == PASSES - 1),
                 )
-            for c in range(0, N, step):
-                nc.scalar.activation(
-                    results[m][:, N * s + c : N * s + c + step], acc[:, c : c + step], GELU, bias=b_cols[:, m : m + 1]
-                )
+            nc.scalar.activation(
+                results[m][:, N * s + c0 : N * s + c0 + width], acc[:], GELU, bias=b_cols[:, m : m + 1]
+            )
 
-        def store(m, c0, c1):
-            nc.sync.dma_start(out=out[P * m : P * m + P, c0:c1], in_=results[m][:, c0:c1])
+        def store(m, c0, c1, queue=nc.sync):
+            queue.dma_start(out=out[P * m : P * m + P, c0:c1], in_=results[m][:, c0:c1])
 
         nc.sync.dma_start(offsets[:], offs)
         for q in range(P // QUAD):
@@ -129,7 +147,10 @@ def tile_list_tab4_gelu_kernel(tc, tab, w, b, offs, out):
                 in_=tab[0, start : start + QUAD * T].rearrange("(r t) -> r t", t=T).bitcast(I32),
             )
         nc.sync.dma_start(out=words[:], in_=tab[0, 0 : 512 * T].rearrange("(p c) -> p c", p=P).bitcast(I32))
-        load_w([0], "early")
+        early = [(0, 0), (0, 1), (1, 0)]
+        raw_tile(early, "early")
+        for k, a in early:
+            load_w(k, a)
 
         nc.vector.memset(warm[:], 0.0)
         nc.scalar.activation(warm[:], warm[:], GELU)
@@ -143,54 +164,63 @@ def tile_list_tab4_gelu_kernel(tc, tab, w, b, offs, out):
         nc.tensor.transpose(b_bank[:, 0:P], b_rows[:], identity[:])
         nc.scalar.copy(b_cols[:], b_bank[:, 0:M_TILES])
 
-        for r in range(S // RUN):
-            picked_scales = keep.tile([P, RUN], U8, name=f"picked_scales{r}", align_bytes=64)
-            cols = slice(r * RUN // 16, (r + 1) * RUN // 16)
-            nc.vector.tensor_copy(picked_scales[:], table_scales[:].indirect(offsets[:, cols]))
-            for h in range(PASSES):
-                nc.sync.dma_start(
-                    out=scales[r][h][0 : MOVED[h], :].bitcast(I32),
-                    in_=picked_scales[SHIFTS[h] : SHIFTS[h] + MOVED[h], :].bitcast(I32),
-                )
+        gather_scales(0)
+        move_scales(0, nc.scalar)
+        gather_scales(1)
 
-        load_w([1, 2], "late")
-        for s in (0, 1):
-            gather_words(s, f"first{s}")
-            part(s)
+        raw_tile([(1, 1), (2, 0), (2, 1)], "late")
+        load_w(1, 1)
+        move_scales(1, nc.sync)
+        load_w(2, 0)
+        load_w(2, 1)
+        gather_words(0, "first")
+        part(0, "parted0")
+        gather_words(1, "even")
+        group_tile([0], "head")
+        group_tile([1], "odd")
         for a in range(PASSES):
             for m in (0, 1):
                 group(nc.scalar.copy, m, a)
-        for m in (0, 1):
-            quantize(m)
+        for a in range(PASSES):
+            quantize(0, a, a + 1)
+        part(1, "head")
+        quantize(1)
         for m in (0, 1):
             product(m, 0)
             product(m, 1)
-            store(m, 0, 2 * N)
-        gather_words(2, "turn0")
-        part(2)
-        prepare(2)
+        store(0, 0, 2 * N)
+        gather_words(2, "odd")
+        part(2, "parted2")
         for m in (0, 1):
             product(m, 2)
-        for s in range(3):
-            product(2, s)
-        store(2, 0, 2 * N)
-        gather_words(3, "turn1")
-        part(3)
-        for m in range(3):
-            product(m, 3)
-            store(m, 2 * N, 4 * N)
-        for m in range(3, M_TILES):
+        store(1, 0, 3 * N)
+        for m, tag in ((2, "even"), (3, "odd")):
+            group_tile([m], tag)
             prepare(m)
-        for m in range(3, M_TILES - 1):
+            for s in range(3):
+                product(m, s)
+            store(m, 0, 3 * N)
+        gather_words(3, "odd")
+        part(3, "parted3")
+        for m in range(4):
+            product(m, 3)
+            store(m, (3 if m else 2) * N, S)
+        group_tile([4, 5, 6, 7], "odd")
+        for m in range(4, M_TILES):
+            prepare(m)
+        for m in range(4, M_TILES - 1):
             for s in range(SLICES):
                 product(m, s)
-            store(m, 0, S)
-        m, half = M_TILES - 1, N // 2
+                if s % 2:
+                    store(m, (s - 1) * N, (s + 1) * N)
+        m = M_TILES - 1
         product(m, 0)
         product(m, 1)
         store(m, 0, 2 * N)
         product(m, 2)
         store(m, 2 * N, 3 * N)
-        product(m, 3, step=half)
-        store(m, 3 * N, 3 * N + half)
-        store(m, 3 * N + half, S)
+        for c0 in range(0, N - P, P):
+            product(m, 3, c0, P)
+        store(m, 3 * N, S - P)
+        product(m, 3, N - P, P)
+        store(m, S - P, S, nc.scalar)

@@ -139,7 +139,7 @@ def tile_list_tab4_gelu_kernel(tc, tab, w, b, offs, out):
             queue.dma_start(out=out[P * m : P * m + P, c0:c1], in_=results[m][:, c0:c1])
 
         nc.sync.dma_start(offsets[:], offs)
-        for q in range(P // QUAD):
+        for q in (0, 2, 1, 3):
             row0 = 4 * q - SHIFTS[0]
             start = 512 * T + T * row0
             nc.sync.dma_start(
@@ -211,8 +211,7 @@ def tile_list_tab4_gelu_kernel(tc, tab, w, b, offs, out):
         for m in range(4, M_TILES - 1):
             for s in range(SLICES):
                 product(m, s)
-                if s % 2:
-                    store(m, (s - 1) * N, (s + 1) * N)
+            store(m, 0, S)
         m = M_TILES - 1
         product(m, 0)
         product(m, 1)

@@ -44,7 +44,6 @@ def tile_list_tab4_gelu_kernel(tc, tab, w, b, offs, out):
         b_rows = keep.tile([P, P], F32, name="b_rows")
         b_cols = keep.tile([P, M_TILES], F32, name="b_cols")
         identity = keep.tile([P, P], F32, name="identity")
-        warm = keep.tile([P, 1], F32, name="warm")
         scales = [
             [keep.tile([P, RUN], U8, name=f"scales{r}{h}", align_bytes=64) for h in range(PASSES)]
             for r in range(S // RUN)
@@ -152,8 +151,6 @@ def tile_list_tab4_gelu_kernel(tc, tab, w, b, offs, out):
         for k, a in early:
             load_w(k, a)
 
-        nc.vector.memset(warm[:], 0.0)
-        nc.scalar.activation(warm[:], warm[:], GELU)
         nc.gpsimd.memset(b_rows[:], 0.0)
         nc.scalar.dma_start(out=b_rows[0:M_TILES, :], in_=b.rearrange("(m p) -> m p", p=P))
         make_identity(nc, identity[:])

@@ -26,96 +26,78 @@ M_TILES = M // P
 N = 512
 SLICES = S // N
 RUN = 1024
-CHUNKS = [(0, 256), (256, 256), (512, 512)]
-
-SHIFTS = (QUAD - 4 - SCALE_ROWS // PASSES, QUAD - 4)
-MOVED = (112, 100)
+HEAD = 256
 
 
 def tile_list_tab4_gelu_kernel(tc, tab, w, b, offs, out):
     nc = tc.nc
     with ExitStack() as ctx:
         keep = ctx.enter_context(tc.tile_pool(name="keep", bufs=1))
+        chain = ctx.enter_context(tc.tile_pool(name="chain", bufs=1))
         psum = ctx.enter_context(tc.psum_pool(name="psum", bufs=8))
 
+        def placed(name, shape, dtype, offset):
+            return chain.tile(shape, dtype, name=name, offset=offset, align_bytes=64)
+
+        Z = 1024
         offsets = keep.tile([P, S // 16], U16, name="offsets")
-        words = keep.tile([P, T], I32, name="words")
-        table_scales = keep.tile([P, T], U8, name="table_scales", tag="late", align_bytes=64)
+        words = keep.tile([P, T], I32, name="words", align_bytes=64)
+        table_scales = keep.tile([P, T], U8, name="table_scales", align_bytes=64)
         b_rows = keep.tile([P, P], F32, name="b_rows")
         b_cols = keep.tile([P, M_TILES], F32, name="b_cols")
         identity = keep.tile([P, P], F32, name="identity")
-        scales = [
-            [keep.tile([P, RUN], U8, name=f"scales{r}{h}", align_bytes=64) for h in range(PASSES)]
-            for r in range(S // RUN)
-        ]
+        warm = keep.tile([P, 8], F32, name="warm")
+        scales = [keep.tile([P, PASSES * RUN], U8, name=f"scales{r}", align_bytes=64) for r in range(S // RUN)]
         results = [keep.tile([P, S], F32, name=f"results{m}") for m in range(M_TILES)]
-        raws, grouped, codes, code_scales, picked, parted, picked_scales = {}, {}, {}, {}, {}, {}, {}
+        grouped = {}
+        raws, codes, code_scales, picked, parted, picked_scales = {}, {}, {}, {}, {}, {}
 
-        def raw_tile(pieces, tag):
-            total = sum(CHUNKS[k][1] for k, a in pieces)
-            raw = keep.tile([P, PACK * total], F32, name=f"raw_{tag}", tag=tag, align_bytes=64)
-            at = 0
-            for k, a in pieces:
-                raws[k, a] = raw[:, at : at + PACK * CHUNKS[k][1]].rearrange("p (i c) -> p i c", i=PACK)
-                at = at + PACK * CHUNKS[k][1]
+        def load_w(raw, a, c0, c1, i0=0, i1=PACK):
+            rows = w[P * PACK * a : P * PACK * (a + 1), c0:c1]
+            nc.sync.dma_start(out=raw[:, i0:i1, :], in_=rows.rearrange("(p i) c -> p i c", i=PACK)[:, i0:i1, :])
+            for m in range(c0 // P, c1 // P):
+                raws[m, a] = raw[:, :, P * m - c0 : P * (m + 1) - c0]
 
-        def load_w(k, a):
-            c0, width = CHUNKS[k]
-            rows = w[P * PACK * a : P * PACK * (a + 1), c0 : c0 + width]
-            nc.sync.dma_start(out=raws[k, a], in_=rows.rearrange("(p i) c -> p i c", i=PACK))
-
-        def gather_scales(r):
-            picked_scales[r] = keep.tile([P, RUN], U8, name=f"picked_scales{r}", align_bytes=64)
+        def gather_scales(r, tile):
+            picked_scales[r] = tile
             cols = slice(r * RUN // 16, (r + 1) * RUN // 16)
-            nc.vector.tensor_copy(picked_scales[r][:], table_scales[:].indirect(offsets[:, cols]))
+            nc.vector.tensor_copy(tile[:], table_scales[:].indirect(offsets[:, cols]))
 
         def move_scales(r, queue):
-            for h in range(PASSES):
+            for q in (0, 2, 1, 3):
                 queue.dma_start(
-                    out=scales[r][h][0 : MOVED[h], :].bitcast(I32),
-                    in_=picked_scales[r][SHIFTS[h] : SHIFTS[h] + MOVED[h], :].bitcast(I32),
+                    out=scales[r][QUAD * q : QUAD * q + 4, :].bitcast(I32),
+                    in_=picked_scales[r][QUAD * q : QUAD * (q + 1) : 4, :].bitcast(I32),
                 )
 
-        def group_tile(tiles, tag):
-            shared = keep.tile([P, len(tiles), PASSES, P, PACK], BF16, name=f"grouped{tiles[0]}", tag=tag, align_bytes=64)
-            for j, m in enumerate(tiles):
-                grouped[m] = shared[:, j]
-
-        def group(copy, m, a):
-            k = max(j for j in range(len(CHUNKS)) if CHUNKS[j][0] <= P * m)
-            c0 = P * m - CHUNKS[k][0]
+        def group(copy, dst, src):
             copy(
-                grouped[m][:, a, :, :].rearrange("p (c j) i -> p c i j", j=PACK),
-                raws[k, a][:, :, c0 : c0 + P].rearrange("p i (c j) -> p c i j", j=PACK),
+                dst.rearrange("p (c j i) -> p c i j", j=PACK, i=PACK),
+                src.rearrange("p i (c j) -> p c i j", j=PACK),
             )
 
-        def quantize(m, a0=0, a1=PASSES):
-            if m not in codes:
-                codes[m] = keep.tile([P, PASSES, P], U32, name=f"codes{m}", align_bytes=64)
-                code_scales[m] = keep.tile([P, PASSES, P], U8, name=f"code_scales{m}", align_bytes=64)
-            nc.vector.quantize_mx(
-                out=codes[m][:, a0:a1, :].rearrange("p a c -> p (a c)").bitcast(E4M3),
-                scales=code_scales[m][:, a0:a1, :].rearrange("p a c -> p (a c)"),
-                in_=grouped[m][:, a0:a1].rearrange("p a c i -> p (a c i)"),
-            )
+        def quantize(src, pieces, words_out=None):
+            m, a = pieces[0]
+            if words_out is None:
+                words_out = keep.tile([P, P * len(pieces)], U32, name=f"codes{m}{a}", align_bytes=64)
+            bytes_out = keep.tile([P, P * len(pieces)], U8, name=f"code_scales{m}{a}", align_bytes=64)
+            nc.vector.quantize_mx(out=words_out[:].bitcast(E4M3), scales=bytes_out[:], in_=src)
+            for j, piece in enumerate(pieces):
+                codes[piece] = words_out[:, P * j : P * (j + 1)]
+                code_scales[piece] = bytes_out[:, P * j : P * (j + 1)]
 
-        def gather_words(s, tag):
-            picked[s] = keep.tile([P, N], I32, name=f"picked_words{s}", tag=tag, align_bytes=64)
+        def gather_words(s, offset):
+            picked[s] = placed(f"picked_words{s}", [P, N], I32, offset)
             cols = slice(s * N // 16, (s + 1) * N // 16)
             nc.vector.tensor_copy(picked[s][:].bitcast(U32), words[:].bitcast(U32).indirect(offsets[:, cols]))
 
-        def part(s, tag):
-            parted[s] = keep.tile([P, PASSES, 2 * N], U8, name=f"parted{s}", tag=tag, align_bytes=64)
+        def part(s):
+            parted[s] = keep.tile([P, PASSES, 2 * N], U8, name=f"parted{s}", align_bytes=64)
             halves = parted[s][:].rearrange("p h c -> p (h c)").bitcast(U16)
             nc.vector.tensor_copy(
                 halves.rearrange("p (h n) -> p h n", h=PASSES),
                 picked[s][:].bitcast(U16).rearrange("p (n h) -> p h n", h=PASSES),
             )
-
-        def prepare(m):
-            for a in range(PASSES):
-                group(nc.vector.tensor_copy, m, a)
-            quantize(m)
 
         def product(m, s, c0=0, width=N):
             acc = psum.tile([P, width], F32, name="acc", tag="acc")
@@ -123,10 +105,10 @@ def tile_list_tab4_gelu_kernel(tc, tab, w, b, offs, out):
             for a in range(PASSES):
                 nc.tensor.matmul_mx(
                     out=acc[:],
-                    lhsT=codes[m][:, a, :].bitcast(E4M3),
-                    lhsT_scale=code_scales[m][:, a, :],
+                    lhsT=codes[m, a].bitcast(E4M3),
+                    lhsT_scale=code_scales[m, a],
                     rhs=parted[s][:, a, 2 * c0 : 2 * (c0 + width)].bitcast(E2M1),
-                    rhs_scale=scales[r][a][:, j0 : j0 + width],
+                    rhs_scale=scales[r][:, RUN * a + j0 : RUN * a + j0 + width],
                     start=(a == 0),
                     stop=(a == PASSES - 1),
                 )
@@ -137,86 +119,111 @@ def tile_list_tab4_gelu_kernel(tc, tab, w, b, offs, out):
         def store(m, c0, c1, queue=nc.sync):
             queue.dma_start(out=out[P * m : P * m + P, c0:c1], in_=results[m][:, c0:c1])
 
-        nc.sync.dma_start(offsets[:], offs)
-        for q in (0, 2, 1, 3):
-            row0 = 4 * q - SHIFTS[0]
-            start = 512 * T + T * row0
-            nc.sync.dma_start(
-                out=table_scales[QUAD * q : QUAD * (q + 1), :].bitcast(I32),
-                in_=tab[0, start : start + QUAD * T].rearrange("(r t) -> r t", t=T).bitcast(I32),
-            )
-        nc.sync.dma_start(out=words[:], in_=tab[0, 0 : 512 * T].rearrange("(p c) -> p c", p=P).bitcast(I32))
-        early = [(0, 0), (0, 1), (1, 0)]
-        raw_tile(early, "early")
-        for k, a in early:
-            load_w(k, a)
+        def raw_tile(name, width):
+            return keep.tile([P, PACK, width], F32, name=name)
 
+        def quantize_tile(m):
+            quantize(grouped[m].rearrange("p a c -> p (a c)"), [(m, 0), (m, 1)])
+
+        nc.gpsimd.memset(table_scales[:, 0 : T // 2].bitcast(I32), 0)
+        nc.vector.memset(table_scales[:, T // 2 : T].bitcast(I32), 0)
+        nc.gpsimd.memset(warm[:], 0.0)
+        nc.scalar.activation(warm[:, 4:5], warm[:, 0:1], GELU)
+        nc.sync.dma_start(offsets[:], offs)
+        head0 = keep.tile([P, PACK, HEAD], F32, name="head0")
+        load_w(head0, 0, 0, HEAD, 0, 2)
+        nc.sync.dma_start(
+            out=table_scales[0:P:4, :].bitcast(I32),
+            in_=tab[0, 512 * T :].rearrange("(h r t) -> r h t", h=PASSES, t=T).bitcast(I32),
+        )
+        load_w(head0, 0, 0, HEAD, 2, 4)
+        nc.sync.dma_start(out=words[:], in_=tab[0, 0 : 512 * T].rearrange("(p c) -> p c", p=P).bitcast(I32))
+        head1 = keep.tile([P, PACK, HEAD], F32, name="head1")
+        load_w(head1, 1, 0, HEAD)
         nc.gpsimd.memset(b_rows[:], 0.0)
         nc.scalar.dma_start(out=b_rows[0:M_TILES, :], in_=b.rearrange("(m p) -> m p", p=P))
         make_identity(nc, identity[:])
         for r in range(S // RUN):
-            for h in range(PASSES):
-                nc.vector.memset(scales[r][h][:].bitcast(I32), 0)
+            nc.gpsimd.memset(scales[r][:].bitcast(I32), 0)
         b_bank = psum.tile([P, N], F32, name="b_bank", tag="acc")
         nc.tensor.transpose(b_bank[:, 0:P], b_rows[:], identity[:])
+
+        grouped0 = keep.tile([P, PACK * HEAD], BF16, name="grouped0", align_bytes=64)
+        group(nc.scalar.copy, grouped0[:], head0[:])
         nc.scalar.copy(b_cols[:], b_bank[:, 0:M_TILES])
-
-        gather_scales(0)
-        move_scales(0, nc.scalar)
-        gather_scales(1)
-
-        raw_tile([(1, 1), (2, 0), (2, 1)], "late")
-        load_w(1, 1)
+        for r in range(S // RUN):
+            gather_scales(r, keep.tile([P, RUN], U8, name=f"picked_scales{r}", align_bytes=64))
+        quantize(grouped0[:], [(0, 0), (1, 0)])
+        warm_bank = psum.tile([P, N], F32, name="warm_bank", tag="acc")
+        for j in range(4):
+            nc.tensor.matmul_mx(
+                out=warm_bank[:],
+                lhsT=codes[0, 0].bitcast(E4M3),
+                lhsT_scale=code_scales[0, 0],
+                rhs=words[:, 0 : N // 2].bitcast(U8).bitcast(E2M1),
+                rhs_scale=table_scales[:, 0:N],
+                start=True,
+                stop=True,
+            )
+        move_scales(0, nc.sync)
+        for a in range(PASSES):
+            load_w(raw_tile(f"second{a}", HEAD), a, HEAD, 2 * HEAD)
         move_scales(1, nc.sync)
-        load_w(2, 0)
-        load_w(2, 1)
-        gather_words(0, "first")
-        part(0, "parted0")
-        gather_words(1, "even")
-        group_tile([0], "head")
-        group_tile([1], "odd")
         for a in range(PASSES):
-            for m in (0, 1):
-                group(nc.scalar.copy, m, a)
-        for a in range(PASSES):
-            quantize(0, a, a + 1)
-        part(1, "head")
-        quantize(1)
+            load_w(raw_tile(f"third{a}", 2 * HEAD), a, 2 * HEAD, M)
+        gather_words(0, 32768)
+        part(0)
+        grouped01 = placed("grouped01", [P, PACK * P], BF16, 4096)
+        grouped11 = keep.tile([P, PACK * P], BF16, name="grouped11", align_bytes=64)
+        group(nc.scalar.copy, grouped01[:], raws[0, 1])
+        group(nc.scalar.copy, grouped11[:], raws[1, 1])
+        quantize(grouped01[:], [(0, 1)])
+        product(0, 0)
+        gather_words(1, 4096 + 64 - 2048)
+        quantize(grouped11[:], [(1, 1)])
+        product(1, 0)
+        part(1)
         for m in (0, 1):
+            product(m, 1)
+            store(m, 0, 2 * N)
+        grouped[2] = placed("grouped_tile2", [P, PASSES, PACK * P], BF16, 5120 - 64)[:]
+        grouped[3] = placed("grouped_tile3", [P, PASSES, PACK * P], BF16, 64)[:]
+        for m in (2, 3):
+            for a in range(PASSES):
+                group(nc.vector.tensor_copy, grouped[m][:, a, :], raws[m, a])
+        for m in (2, 3):
+            quantize_tile(m)
             product(m, 0)
             product(m, 1)
-        store(0, 0, 2 * N)
-        gather_words(2, "odd")
-        part(2, "parted2")
-        for m in (0, 1):
+            store(m, 0, 2 * N)
+        gather_words(2, 5120 - 64)
+        part(2)
+        gather_words(3, 5120 - 64)
+        part(3)
+        for m in range(3):
             product(m, 2)
-        store(1, 0, 3 * N)
-        for m, tag in ((2, "even"), (3, "odd")):
-            group_tile([m], tag)
-            prepare(m)
-            for s in range(3):
-                product(m, s)
-            store(m, 0, 3 * N)
-        gather_words(3, "odd")
-        part(3, "parted3")
-        for m in range(4):
+            store(m, 2 * N, 3 * N)
+        product(3, 2)
+        product(3, 3)
+        store(3, 2 * N, S)
+        for m in range(3):
             product(m, 3)
-            store(m, (3 if m else 2) * N, S)
-        group_tile([4, 5, 6, 7], "odd")
+            store(m, 3 * N, S)
         for m in range(4, M_TILES):
-            prepare(m)
+            grouped[m] = placed(f"grouped_tile{m}", [P, PASSES, PACK * P], BF16, 8192 + 2048 * m)[:]
+            for a in range(PASSES):
+                group(nc.vector.tensor_copy, grouped[m][:, a, :], raws[m, a])
+            quantize_tile(m)
         for m in range(4, M_TILES - 1):
             for s in range(SLICES):
                 product(m, s)
-            store(m, 0, S)
+                if s % 2:
+                    store(m, (s - 1) * N, (s + 1) * N)
         m = M_TILES - 1
         product(m, 0)
         product(m, 1)
         store(m, 0, 2 * N)
         product(m, 2)
         store(m, 2 * N, 3 * N)
-        for c0 in range(0, N - P, P):
-            product(m, 3, c0, P)
-        store(m, 3 * N, S - P)
-        product(m, 3, N - P, P)
-        store(m, S - P, S, nc.scalar)
+        product(m, 3)
+        store(m, 3 * N, S, nc.scalar)

@@ -20,54 +20,63 @@ P = 128
 QUAD = 32
 PACK = 4
 PASSES = K // (P * PACK)
-SCALE_ROWS = K // 32
 M_TILES = M // P
 
 N = 512
 SLICES = S // N
 RUN = 1024
 HEAD = 256
+SPREAD = 4
+
+OVERLAP = 64
+HINGE = 4 * N
+BELOW = HINGE + OVERLAP - 4 * N
+ABOVE = HINGE + 2 * PACK * P - OVERLAP
 
 
 def tile_list_tab4_gelu_kernel(tc, tab, w, b, offs, out):
     nc = tc.nc
     with ExitStack() as ctx:
         keep = ctx.enter_context(tc.tile_pool(name="keep", bufs=1))
-        chain = ctx.enter_context(tc.tile_pool(name="chain", bufs=1))
+        shared = ctx.enter_context(tc.tile_pool(name="shared", bufs=1))
         psum = ctx.enter_context(tc.psum_pool(name="psum", bufs=8))
 
-        def placed(name, shape, dtype, offset):
-            return chain.tile(shape, dtype, name=name, offset=offset, align_bytes=64)
+        def tile(name, shape, dtype, offset=None):
+            if offset is None:
+                return keep.tile(shape, dtype, name=name, align_bytes=64)
+            return shared.tile(shape, dtype, name=name, offset=offset, align_bytes=64)
 
-        Z = 1024
         offsets = keep.tile([P, S // 16], U16, name="offsets")
-        words = keep.tile([P, T], I32, name="words", align_bytes=64)
-        table_scales = keep.tile([P, T], U8, name="table_scales", align_bytes=64)
-        b_rows = keep.tile([P, P], F32, name="b_rows")
-        b_cols = keep.tile([P, M_TILES], F32, name="b_cols")
-        identity = keep.tile([P, P], F32, name="identity")
-        warm = keep.tile([P, 8], F32, name="warm")
-        scales = [keep.tile([P, PASSES * RUN], U8, name=f"scales{r}", align_bytes=64) for r in range(S // RUN)]
-        results = [keep.tile([P, S], F32, name=f"results{m}") for m in range(M_TILES)]
-        grouped = {}
-        raws, codes, code_scales, picked, parted, picked_scales = {}, {}, {}, {}, {}, {}
+        words = tile("words", [P, T], I32)
+        table_scales = tile("table_scales", [P, T], U8)
+        scales = [tile(f"scales{r}", [P, PASSES * RUN], U8) for r in range(S // RUN)]
+        b_rows = tile("b_rows", [P, P], F32)
+        b_cols = tile("b_cols", [P, M_TILES], F32)
+        identity = tile("identity", [P, P], F32)
+        results = [tile(f"results{m}", [P, S], F32) for m in range(M_TILES)]
+        raws, codes, code_scales, picked_words, parted, picked_scales = {}, {}, {}, {}, {}, {}
 
-        def load_w(raw, a, c0, c1, i0=0, i1=PACK):
-            rows = w[P * PACK * a : P * PACK * (a + 1), c0:c1]
-            nc.sync.dma_start(out=raw[:, i0:i1, :], in_=rows.rearrange("(p i) c -> p i c", i=PACK)[:, i0:i1, :])
-            for m in range(c0 // P, c1 // P):
-                raws[m, a] = raw[:, :, P * m - c0 : P * (m + 1) - c0]
+        def load_w(raw, a, c0, i0=0, i1=PACK):
+            width = raw.shape[2]
+            rows = w[P * PACK * a : P * PACK * (a + 1), c0 : c0 + width].rearrange("(p i) c -> p i c", i=PACK)
+            nc.sync.dma_start(out=raw[:, i0:i1, :], in_=rows[:, i0:i1, :])
+            for j in range(width // P):
+                raws[c0 // P + j, a] = raw[:, :, P * j : P * (j + 1)]
 
-        def gather_scales(r, tile):
-            picked_scales[r] = tile
+        def load_chunk(c0, width):
+            for a in range(PASSES):
+                load_w(tile(f"raw{c0}_{a}", [P, PACK, width], F32), a, c0)
+
+        def gather_scales(r):
+            picked_scales[r] = tile(f"picked_scales{r}", [P, RUN], U8)
             cols = slice(r * RUN // 16, (r + 1) * RUN // 16)
-            nc.vector.tensor_copy(tile[:], table_scales[:].indirect(offsets[:, cols]))
+            nc.vector.tensor_copy(picked_scales[r][:], table_scales[:].indirect(offsets[:, cols]))
 
-        def move_scales(r, queue):
+        def move_scales(r):
             for q in (0, 2, 1, 3):
-                queue.dma_start(
+                nc.sync.dma_start(
                     out=scales[r][QUAD * q : QUAD * q + 4, :].bitcast(I32),
-                    in_=picked_scales[r][QUAD * q : QUAD * (q + 1) : 4, :].bitcast(I32),
+                    in_=picked_scales[r][QUAD * q : QUAD * (q + 1) : SPREAD, :].bitcast(I32),
                 )
 
         def group(copy, dst, src):
@@ -76,70 +85,68 @@ def tile_list_tab4_gelu_kernel(tc, tab, w, b, offs, out):
                 src.rearrange("p i (c j) -> p c i j", j=PACK),
             )
 
-        def quantize(src, pieces, words_out=None):
+        def quantize(src, pieces):
             m, a = pieces[0]
-            if words_out is None:
-                words_out = keep.tile([P, P * len(pieces)], U32, name=f"codes{m}{a}", align_bytes=64)
-            bytes_out = keep.tile([P, P * len(pieces)], U8, name=f"code_scales{m}{a}", align_bytes=64)
-            nc.vector.quantize_mx(out=words_out[:].bitcast(E4M3), scales=bytes_out[:], in_=src)
+            piece_codes = tile(f"codes{m}{a}", [P, P * len(pieces)], U32)
+            piece_scales = tile(f"code_scales{m}{a}", [P, P * len(pieces)], U8)
+            nc.vector.quantize_mx(out=piece_codes[:].bitcast(E4M3), scales=piece_scales[:], in_=src)
             for j, piece in enumerate(pieces):
-                codes[piece] = words_out[:, P * j : P * (j + 1)]
-                code_scales[piece] = bytes_out[:, P * j : P * (j + 1)]
+                codes[piece] = piece_codes[:, P * j : P * (j + 1)]
+                code_scales[piece] = piece_scales[:, P * j : P * (j + 1)]
 
-        def gather_words(s, offset):
-            picked[s] = placed(f"picked_words{s}", [P, N], I32, offset)
+        def group_tile(m, offset=None):
+            grouped = tile(f"grouped{m}", [P, PASSES, PACK * P], BF16, offset)
+            for a in range(PASSES):
+                group(nc.vector.tensor_copy, grouped[:, a, :], raws[m, a])
+            return grouped
+
+        def quantize_tile(m, grouped):
+            quantize(grouped[:].rearrange("p a c -> p (a c)"), [(m, a) for a in range(PASSES)])
+
+        def gather_words(s, offset=None):
+            picked_words[s] = tile(f"picked_words{s}", [P, N], I32, offset)
             cols = slice(s * N // 16, (s + 1) * N // 16)
-            nc.vector.tensor_copy(picked[s][:].bitcast(U32), words[:].bitcast(U32).indirect(offsets[:, cols]))
+            nc.vector.tensor_copy(picked_words[s][:].bitcast(U32), words[:].bitcast(U32).indirect(offsets[:, cols]))
 
         def part(s):
-            parted[s] = keep.tile([P, PASSES, 2 * N], U8, name=f"parted{s}", align_bytes=64)
-            halves = parted[s][:].rearrange("p h c -> p (h c)").bitcast(U16)
+            parted[s] = tile(f"parted{s}", [P, PASSES, 2 * N], U8)
+            halves = parted[s][:].rearrange("p a c -> p (a c)").bitcast(U16)
             nc.vector.tensor_copy(
-                halves.rearrange("p (h n) -> p h n", h=PASSES),
-                picked[s][:].bitcast(U16).rearrange("p (n h) -> p h n", h=PASSES),
+                halves.rearrange("p (a n) -> p a n", a=PASSES),
+                picked_words[s][:].bitcast(U16).rearrange("p (n a) -> p a n", a=PASSES),
             )
 
-        def product(m, s, c0=0, width=N):
-            acc = psum.tile([P, width], F32, name="acc", tag="acc")
-            r, j0 = divmod(N * s + c0, RUN)
+        def product(m, s):
+            acc = psum.tile([P, N], F32, name="acc", tag="acc")
+            r, j0 = divmod(N * s, RUN)
             for a in range(PASSES):
                 nc.tensor.matmul_mx(
                     out=acc[:],
                     lhsT=codes[m, a].bitcast(E4M3),
                     lhsT_scale=code_scales[m, a],
-                    rhs=parted[s][:, a, 2 * c0 : 2 * (c0 + width)].bitcast(E2M1),
-                    rhs_scale=scales[r][:, RUN * a + j0 : RUN * a + j0 + width],
+                    rhs=parted[s][:, a, :].bitcast(E2M1),
+                    rhs_scale=scales[r][:, RUN * a + j0 : RUN * a + j0 + N],
                     start=(a == 0),
                     stop=(a == PASSES - 1),
                 )
-            nc.scalar.activation(
-                results[m][:, N * s + c0 : N * s + c0 + width], acc[:], GELU, bias=b_cols[:, m : m + 1]
-            )
+            nc.scalar.activation(results[m][:, N * s : N * (s + 1)], acc[:], GELU, bias=b_cols[:, m : m + 1])
 
-        def store(m, c0, c1, queue=nc.sync):
-            queue.dma_start(out=out[P * m : P * m + P, c0:c1], in_=results[m][:, c0:c1])
-
-        def raw_tile(name, width):
-            return keep.tile([P, PACK, width], F32, name=name)
-
-        def quantize_tile(m):
-            quantize(grouped[m].rearrange("p a c -> p (a c)"), [(m, 0), (m, 1)])
+        def store(m, s0, s1, queue=nc.sync):
+            queue.dma_start(out=out[P * m : P * (m + 1), N * s0 : N * s1], in_=results[m][:, N * s0 : N * s1])
 
         nc.gpsimd.memset(table_scales[:, 0 : T // 2].bitcast(I32), 0)
         nc.vector.memset(table_scales[:, T // 2 : T].bitcast(I32), 0)
-        nc.gpsimd.memset(warm[:], 0.0)
-        nc.scalar.activation(warm[:, 4:5], warm[:, 0:1], GELU)
         nc.sync.dma_start(offsets[:], offs)
-        head0 = keep.tile([P, PACK, HEAD], F32, name="head0")
-        load_w(head0, 0, 0, HEAD, 0, 2)
+        head0 = tile("head0", [P, PACK, HEAD], F32)
+        load_w(head0, 0, 0, 0, PACK // 2)
         nc.sync.dma_start(
-            out=table_scales[0:P:4, :].bitcast(I32),
-            in_=tab[0, 512 * T :].rearrange("(h r t) -> r h t", h=PASSES, t=T).bitcast(I32),
+            out=table_scales[0:P:SPREAD, :].bitcast(I32),
+            in_=tab[0, 4 * P * T :].rearrange("(a g t) -> g a t", a=PASSES, t=T).bitcast(I32),
         )
-        load_w(head0, 0, 0, HEAD, 2, 4)
-        nc.sync.dma_start(out=words[:], in_=tab[0, 0 : 512 * T].rearrange("(p c) -> p c", p=P).bitcast(I32))
-        head1 = keep.tile([P, PACK, HEAD], F32, name="head1")
-        load_w(head1, 1, 0, HEAD)
+        load_w(head0, 0, 0, PACK // 2, PACK)
+        nc.sync.dma_start(out=words[:], in_=tab[0, 0 : 4 * P * T].rearrange("(p c) -> p c", p=P).bitcast(I32))
+        load_w(tile("head1", [P, PACK, HEAD], F32), 1, 0)
+
         nc.gpsimd.memset(b_rows[:], 0.0)
         nc.scalar.dma_start(out=b_rows[0:M_TILES, :], in_=b.rearrange("(m p) -> m p", p=P))
         make_identity(nc, identity[:])
@@ -148,82 +155,64 @@ def tile_list_tab4_gelu_kernel(tc, tab, w, b, offs, out):
         b_bank = psum.tile([P, N], F32, name="b_bank", tag="acc")
         nc.tensor.transpose(b_bank[:, 0:P], b_rows[:], identity[:])
 
-        grouped0 = keep.tile([P, PACK * HEAD], BF16, name="grouped0", align_bytes=64)
-        group(nc.scalar.copy, grouped0[:], head0[:])
+        grouped_head0 = tile("grouped_head0", [P, PACK * HEAD], BF16)
+        group(nc.scalar.copy, grouped_head0[:], head0[:])
         nc.scalar.copy(b_cols[:], b_bank[:, 0:M_TILES])
         for r in range(S // RUN):
-            gather_scales(r, keep.tile([P, RUN], U8, name=f"picked_scales{r}", align_bytes=64))
-        quantize(grouped0[:], [(0, 0), (1, 0)])
-        warm_bank = psum.tile([P, N], F32, name="warm_bank", tag="acc")
-        for j in range(4):
-            nc.tensor.matmul_mx(
-                out=warm_bank[:],
-                lhsT=codes[0, 0].bitcast(E4M3),
-                lhsT_scale=code_scales[0, 0],
-                rhs=words[:, 0 : N // 2].bitcast(U8).bitcast(E2M1),
-                rhs_scale=table_scales[:, 0:N],
-                start=True,
-                stop=True,
-            )
-        move_scales(0, nc.sync)
-        for a in range(PASSES):
-            load_w(raw_tile(f"second{a}", HEAD), a, HEAD, 2 * HEAD)
-        move_scales(1, nc.sync)
-        for a in range(PASSES):
-            load_w(raw_tile(f"third{a}", 2 * HEAD), a, 2 * HEAD, M)
-        gather_words(0, 32768)
+            gather_scales(r)
+        quantize(grouped_head0[:], [(0, 0), (1, 0)])
+        move_scales(0)
+        load_chunk(HEAD, HEAD)
+        move_scales(1)
+        load_chunk(2 * HEAD, M - 2 * HEAD)
+
+        gather_words(0)
         part(0)
-        grouped01 = placed("grouped01", [P, PACK * P], BF16, 4096)
-        grouped11 = keep.tile([P, PACK * P], BF16, name="grouped11", align_bytes=64)
-        group(nc.scalar.copy, grouped01[:], raws[0, 1])
+        hinge = tile("hinge", [P, PACK * P], BF16, HINGE)
+        grouped11 = tile("grouped11", [P, PACK * P], BF16)
+        group(nc.scalar.copy, hinge[:], raws[0, 1])
         group(nc.scalar.copy, grouped11[:], raws[1, 1])
-        quantize(grouped01[:], [(0, 1)])
+        quantize(hinge[:], [(0, 1)])
         product(0, 0)
-        gather_words(1, 4096 + 64 - 2048)
+        gather_words(1, BELOW)
         quantize(grouped11[:], [(1, 1)])
         product(1, 0)
         part(1)
         for m in (0, 1):
             product(m, 1)
-            store(m, 0, 2 * N)
-        grouped[2] = placed("grouped_tile2", [P, PASSES, PACK * P], BF16, 5120 - 64)[:]
-        grouped[3] = placed("grouped_tile3", [P, PASSES, PACK * P], BF16, 64)[:]
+            store(m, 0, 2)
+
+        second = {2: group_tile(2, ABOVE), 3: group_tile(3)}
         for m in (2, 3):
-            for a in range(PASSES):
-                group(nc.vector.tensor_copy, grouped[m][:, a, :], raws[m, a])
-        for m in (2, 3):
-            quantize_tile(m)
+            quantize_tile(m, second[m])
             product(m, 0)
             product(m, 1)
-            store(m, 0, 2 * N)
-        gather_words(2, 5120 - 64)
-        part(2)
-        gather_words(3, 5120 - 64)
-        part(3)
+            store(m, 0, 2)
+        for s in (2, 3):
+            gather_words(s, ABOVE)
+            part(s)
         for m in range(3):
             product(m, 2)
-            store(m, 2 * N, 3 * N)
+            store(m, 2, 3)
         product(3, 2)
         product(3, 3)
-        store(3, 2 * N, S)
+        store(3, 2, SLICES)
         for m in range(3):
             product(m, 3)
-            store(m, 3 * N, S)
+            store(m, 3, SLICES)
+
         for m in range(4, M_TILES):
-            grouped[m] = placed(f"grouped_tile{m}", [P, PASSES, PACK * P], BF16, 8192 + 2048 * m)[:]
-            for a in range(PASSES):
-                group(nc.vector.tensor_copy, grouped[m][:, a, :], raws[m, a])
-            quantize_tile(m)
+            quantize_tile(m, group_tile(m))
         for m in range(4, M_TILES - 1):
-            for s in range(SLICES):
+            for s in range(0, SLICES, 2):
                 product(m, s)
-                if s % 2:
-                    store(m, (s - 1) * N, (s + 1) * N)
+                product(m, s + 1)
+                store(m, s, s + 2)
         m = M_TILES - 1
         product(m, 0)
         product(m, 1)
-        store(m, 0, 2 * N)
+        store(m, 0, 2)
         product(m, 2)
-        store(m, 2 * N, 3 * N)
+        store(m, 2, 3)
         product(m, 3)
-        store(m, 3 * N, S, nc.scalar)
+        store(m, 3, SLICES, nc.scalar)

@@ -53,7 +53,7 @@ def tile_list_tab4_gelu_kernel(tc, tab, w, b, offs, out):
         b_rows = tile("b_rows", [P, P], F32)
         b_cols = tile("b_cols", [P, M_TILES], F32)
         identity = tile("identity", [P, P], F32)
-        results = [tile(f"results{m}", [P, S], F32) for m in range(M_TILES)]
+        results = tile("results", [P, M_TILES, S], F32)
         raws, codes, code_scales, picked_words, parted, picked_scales = {}, {}, {}, {}, {}, {}
 
         def load_w(raw, a, c0, i0=0, i1=PACK):
@@ -129,10 +129,11 @@ def tile_list_tab4_gelu_kernel(tc, tab, w, b, offs, out):
                     start=(a == 0),
                     stop=(a == PASSES - 1),
                 )
-            nc.scalar.activation(results[m][:, N * s : N * (s + 1)], acc[:], GELU, bias=b_cols[:, m : m + 1])
+            nc.scalar.activation(results[:, m, N * s : N * (s + 1)], acc[:], GELU, bias=b_cols[:, m : m + 1])
 
-        def store(m, s0, s1, queue=nc.sync):
-            queue.dma_start(out=out[P * m : P * (m + 1), N * s0 : N * s1], in_=results[m][:, N * s0 : N * s1])
+        def store(m0, m1, s0, s1, queue=nc.sync):
+            rows = out[P * m0 : P * m1, N * s0 : N * s1].rearrange("(m p) c -> p m c", p=P)
+            queue.dma_start(out=rows, in_=results[:, m0:m1, N * s0 : N * s1])
 
         nc.gpsimd.memset(table_scales[:, 0 : T // 2].bitcast(I32), 0)
         nc.vector.memset(table_scales[:, T // 2 : T].bitcast(I32), 0)
@@ -180,39 +181,32 @@ def tile_list_tab4_gelu_kernel(tc, tab, w, b, offs, out):
         part(1)
         for m in (0, 1):
             product(m, 1)
-            store(m, 0, 2)
+        store(0, 2, 0, 2)
 
         second = {2: group_tile(2, ABOVE), 3: group_tile(3)}
         for m in (2, 3):
             quantize_tile(m, second[m])
             product(m, 0)
             product(m, 1)
-            store(m, 0, 2)
+        store(2, 4, 0, 2)
         for s in (2, 3):
             gather_words(s, ABOVE)
             part(s)
-        for m in range(3):
-            product(m, 2)
-            store(m, 2, 3)
-        product(3, 2)
-        product(3, 3)
-        store(3, 2, SLICES)
-        for m in range(3):
-            product(m, 3)
-            store(m, 3, SLICES)
+        for s in (2, 3):
+            for m in range(4):
+                product(m, s)
+            store(0, 4, s, s + 1)
 
         for m in range(4, M_TILES):
             quantize_tile(m, group_tile(m))
         for m in range(4, M_TILES - 1):
-            for s in range(0, SLICES, 2):
+            for s in range(SLICES):
                 product(m, s)
-                product(m, s + 1)
-                store(m, s, s + 2)
+            store(m, m + 1, 0, SLICES)
         m = M_TILES - 1
         product(m, 0)
         product(m, 1)
-        store(m, 0, 2)
+        store(m, m + 1, 0, 2)
         product(m, 2)
-        store(m, 2, 3)
         product(m, 3)
-        store(m, 3, SLICES, nc.scalar)
+        store(m, m + 1, 2, SLICES, nc.scalar)

@@ -26,7 +26,7 @@ N = 512
 SLICES = S // N
 RUN = 1024
 HEAD = 256
-SPREAD = 4
+ROWS0 = P - QUAD
 
 OVERLAP = 64
 HINGE = 4 * N
@@ -56,10 +56,10 @@ def tile_list_tab4_gelu_kernel(tc, tab, w, b, offs, out):
         results = tile("results", [P, M_TILES, S], F32)
         raws, codes, code_scales, picked_words, parted, picked_scales = {}, {}, {}, {}, {}, {}
 
-        def load_w(raw, a, c0, i0=0, i1=PACK):
+        def load_w(raw, a, c0):
             width = raw.shape[2]
             rows = w[P * PACK * a : P * PACK * (a + 1), c0 : c0 + width].rearrange("(p i) c -> p i c", i=PACK)
-            nc.sync.dma_start(out=raw[:, i0:i1, :], in_=rows[:, i0:i1, :])
+            nc.sync.dma_start(out=raw[:], in_=rows)
             for j in range(width // P):
                 raws[c0 // P + j, a] = raw[:, :, P * j : P * (j + 1)]
 
@@ -76,7 +76,7 @@ def tile_list_tab4_gelu_kernel(tc, tab, w, b, offs, out):
             for q in (0, 2, 1, 3):
                 nc.sync.dma_start(
                     out=scales[r][QUAD * q : QUAD * q + 4, :].bitcast(I32),
-                    in_=picked_scales[r][QUAD * q : QUAD * (q + 1) : SPREAD, :].bitcast(I32),
+                    in_=picked_scales[r][ROWS0 + 8 * q : ROWS0 + 8 * (q + 1), :].bitcast(I32),
                 )
 
         def group(copy, dst, src):
@@ -108,8 +108,8 @@ def tile_list_tab4_gelu_kernel(tc, tab, w, b, offs, out):
             cols = slice(s * N // 16, (s + 1) * N // 16)
             nc.vector.tensor_copy(picked_words[s][:].bitcast(U32), words[:].bitcast(U32).indirect(offsets[:, cols]))
 
-        def part(s):
-            parted[s] = tile(f"parted{s}", [P, PASSES, 2 * N], U8)
+        def part(s, offset=None):
+            parted[s] = tile(f"parted{s}", [P, PASSES, 2 * N], U8, offset)
             halves = parted[s][:].rearrange("p a c -> p (a c)").bitcast(U16)
             nc.vector.tensor_copy(
                 halves.rearrange("p (a n) -> p a n", a=PASSES),
@@ -135,78 +135,84 @@ def tile_list_tab4_gelu_kernel(tc, tab, w, b, offs, out):
             rows = out[P * m0 : P * m1, N * s0 : N * s1].rearrange("(m p) c -> p m c", p=P)
             queue.dma_start(out=rows, in_=results[:, m0:m1, N * s0 : N * s1])
 
-        nc.gpsimd.memset(table_scales[:, 0 : T // 2].bitcast(I32), 0)
-        nc.vector.memset(table_scales[:, T // 2 : T].bitcast(I32), 0)
+        nc.vector.memset(table_scales[0:ROWS0, :].bitcast(I32), 0)
         nc.sync.dma_start(offsets[:], offs)
-        head0 = tile("head0", [P, PACK, HEAD], F32)
-        load_w(head0, 0, 0, 0, PACK // 2)
         nc.sync.dma_start(
-            out=table_scales[0:P:SPREAD, :].bitcast(I32),
+            out=table_scales[ROWS0:P, :].bitcast(I32),
             in_=tab[0, 4 * P * T :].rearrange("(a g t) -> g a t", a=PASSES, t=T).bitcast(I32),
         )
-        load_w(head0, 0, 0, PACK // 2, PACK)
         nc.sync.dma_start(out=words[:], in_=tab[0, 0 : 4 * P * T].rearrange("(p c) -> p c", p=P).bitcast(I32))
-        load_w(tile("head1", [P, PACK, HEAD], F32), 1, 0)
+        head0 = tile("head0", [P, PACK, HEAD], F32)
+        load_w(head0, 0, 0)
 
-        nc.gpsimd.memset(b_rows[:], 0.0)
-        nc.scalar.dma_start(out=b_rows[0:M_TILES, :], in_=b.rearrange("(m p) -> m p", p=P))
+        nc.scalar.dma_start(out=b_rows[P - M_TILES : P, :], in_=b.rearrange("(m p) -> m p", p=P))
         make_identity(nc, identity[:])
+        nc.scalar.activation(b_rows[0 : P - M_TILES, :], identity[0 : P - M_TILES, :], GELU, scale=0.0)
         for r in range(S // RUN):
             nc.gpsimd.memset(scales[r][:].bitcast(I32), 0)
         b_bank = psum.tile([P, N], F32, name="b_bank", tag="acc")
         nc.tensor.transpose(b_bank[:, 0:P], b_rows[:], identity[:])
+        nc.scalar.copy(b_cols[:], b_bank[:, P - M_TILES : P])
 
-        grouped_head0 = tile("grouped_head0", [P, PACK * HEAD], BF16)
-        group(nc.scalar.copy, grouped_head0[:], head0[:])
-        nc.scalar.copy(b_cols[:], b_bank[:, 0:M_TILES])
         for r in range(S // RUN):
             gather_scales(r)
-        quantize(grouped_head0[:], [(0, 0), (1, 0)])
         move_scales(0)
+        load_w(tile("head1", [P, PACK, HEAD], F32), 1, 0)
         load_chunk(HEAD, HEAD)
         move_scales(1)
         load_chunk(2 * HEAD, M - 2 * HEAD)
 
-        gather_words(0)
-        part(0)
+        grouped_head0 = tile("grouped_head0", [P, PACK * HEAD], BF16)
         hinge = tile("hinge", [P, PACK * P], BF16, HINGE)
         grouped11 = tile("grouped11", [P, PACK * P], BF16)
+        group(nc.scalar.copy, grouped_head0[:], head0[:])
         group(nc.scalar.copy, hinge[:], raws[0, 1])
         group(nc.scalar.copy, grouped11[:], raws[1, 1])
+        gather_words(0)
+        part(0)
+        gather_words(1)
+        quantize(grouped_head0[:], [(0, 0), (1, 0)])
         quantize(hinge[:], [(0, 1)])
         product(0, 0)
-        gather_words(1, BELOW)
+        part(1, BELOW)
         quantize(grouped11[:], [(1, 1)])
+        product(0, 1)
+        store(0, 1, 0, 2)
         product(1, 0)
-        part(1)
-        for m in (0, 1):
-            product(m, 1)
-        store(0, 2, 0, 2)
+        product(1, 1)
+        store(1, 2, 0, 2)
 
         second = {2: group_tile(2, ABOVE), 3: group_tile(3)}
         for m in (2, 3):
             quantize_tile(m, second[m])
             product(m, 0)
             product(m, 1)
-        store(2, 4, 0, 2)
+            store(m, m + 1, 0, 2)
         for s in (2, 3):
             gather_words(s, ABOVE)
             part(s)
-        for s in (2, 3):
-            for m in range(4):
-                product(m, s)
-            store(0, 4, s, s + 1)
+        for m in range(3):
+            product(m, 2)
+            store(m, m + 1, 2, 3)
+        product(3, 2)
+        product(3, 3)
+        store(3, 4, 2, SLICES)
+        for m in range(3):
+            product(m, 3)
+            store(m, m + 1, 3, SLICES)
 
         for m in range(4, M_TILES):
             quantize_tile(m, group_tile(m))
         for m in range(4, M_TILES - 1):
-            for s in range(SLICES):
+            for s in range(0, SLICES, 2):
                 product(m, s)
-            store(m, m + 1, 0, SLICES)
+                product(m, s + 1)
+                store(m, m + 1, s, s + 2)
         m = M_TILES - 1
         product(m, 0)
         product(m, 1)
         store(m, m + 1, 0, 2)
         product(m, 2)
+        store(m, m + 1, 2, 3)
         product(m, 3)
-        store(m, m + 1, 2, SLICES, nc.scalar)
+        store(m, m + 1, 3, SLICES, nc.scalar)

@@ -28,10 +28,12 @@ RUN = 1024
 HEAD = 256
 ROWS0 = P - QUAD
 
-OVERLAP = 64
-HINGE = 4 * N
-BELOW = HINGE + OVERLAP - 4 * N
-ABOVE = HINGE + 2 * PACK * P - OVERLAP
+SLICE = 4 * N
+RAW = 4 * PACK * HEAD
+FIRST = 0
+THIRD = FIRST + SLICE
+LAST = 3 * 4 * N
+SECOND = THIRD + 6 * LAST
 
 
 def tile_list_tab4_gelu_kernel(tc, tab, w, b, offs, out):
@@ -63,9 +65,9 @@ def tile_list_tab4_gelu_kernel(tc, tab, w, b, offs, out):
             for j in range(width // P):
                 raws[c0 // P + j, a] = raw[:, :, P * j : P * (j + 1)]
 
-        def load_chunk(c0, width):
+        def load_chunk(c0, width, offset=None):
             for a in range(PASSES):
-                load_w(tile(f"raw{c0}_{a}", [P, PACK, width], F32), a, c0)
+                load_w(tile(f"raw{c0}_{a}", [P, PACK, width], F32, offset if a else None), a, c0)
 
         def gather_scales(r):
             picked_scales[r] = tile(f"picked_scales{r}", [P, RUN], U8)
@@ -85,9 +87,9 @@ def tile_list_tab4_gelu_kernel(tc, tab, w, b, offs, out):
                 src.rearrange("p i (c j) -> p c i j", j=PACK),
             )
 
-        def quantize(src, pieces):
+        def quantize(src, pieces, offset=None):
             m, a = pieces[0]
-            piece_codes = tile(f"codes{m}{a}", [P, P * len(pieces)], U32)
+            piece_codes = tile(f"codes{m}{a}", [P, P * len(pieces)], U32, offset)
             piece_scales = tile(f"code_scales{m}{a}", [P, P * len(pieces)], U8)
             nc.vector.quantize_mx(out=piece_codes[:].bitcast(E4M3), scales=piece_scales[:], in_=src)
             for j, piece in enumerate(pieces):
@@ -100,8 +102,8 @@ def tile_list_tab4_gelu_kernel(tc, tab, w, b, offs, out):
                 group(nc.vector.tensor_copy, grouped[:, a, :], raws[m, a])
             return grouped
 
-        def quantize_tile(m, grouped):
-            quantize(grouped[:].rearrange("p a c -> p (a c)"), [(m, a) for a in range(PASSES)])
+        def quantize_tile(m, grouped, offset=None):
+            quantize(grouped[:].rearrange("p a c -> p (a c)"), [(m, a) for a in range(PASSES)], offset)
 
         def gather_words(s, offset=None):
             picked_words[s] = tile(f"picked_words{s}", [P, N], I32, offset)
@@ -116,20 +118,23 @@ def tile_list_tab4_gelu_kernel(tc, tab, w, b, offs, out):
                 picked_words[s][:].bitcast(U16).rearrange("p (n a) -> p a n", a=PASSES),
             )
 
-        def product(m, s):
-            acc = psum.tile([P, N], F32, name="acc", tag="acc")
-            r, j0 = divmod(N * s, RUN)
+        def products(*pieces, into=None):
+            banks = [psum.tile([P, N], F32, name="acc", tag="acc") for piece in pieces]
             for a in range(PASSES):
-                nc.tensor.matmul_mx(
-                    out=acc[:],
-                    lhsT=codes[m, a].bitcast(E4M3),
-                    lhsT_scale=code_scales[m, a],
-                    rhs=parted[s][:, a, :].bitcast(E2M1),
-                    rhs_scale=scales[r][:, RUN * a + j0 : RUN * a + j0 + N],
-                    start=(a == 0),
-                    stop=(a == PASSES - 1),
-                )
-            nc.scalar.activation(results[:, m, N * s : N * (s + 1)], acc[:], GELU, bias=b_cols[:, m : m + 1])
+                for (m, s), acc in zip(pieces, banks):
+                    r, j0 = divmod(N * s, RUN)
+                    nc.tensor.matmul_mx(
+                        out=acc[:],
+                        lhsT=codes[m, a].bitcast(E4M3),
+                        lhsT_scale=code_scales[m, a],
+                        rhs=parted[s][:, a, :].bitcast(E2M1),
+                        rhs_scale=scales[r][:, RUN * a + j0 : RUN * a + j0 + N],
+                        start=(a == 0),
+                        stop=(a == PASSES - 1),
+                    )
+            for j, ((m, s), acc) in enumerate(zip(pieces, banks)):
+                dst = results[:, m, N * s : N * (s + 1)] if into is None else into[:, j, :]
+                nc.scalar.activation(dst, acc[:], GELU, bias=b_cols[:, m : m + 1])
 
         def store(m0, m1, s0, s1, queue=nc.sync):
             rows = out[P * m0 : P * m1, N * s0 : N * s1].rearrange("(m p) c -> p m c", p=P)
@@ -156,63 +161,62 @@ def tile_list_tab4_gelu_kernel(tc, tab, w, b, offs, out):
 
         for r in range(S // RUN):
             gather_scales(r)
-        move_scales(0)
         load_w(tile("head1", [P, PACK, HEAD], F32), 1, 0)
-        load_chunk(HEAD, HEAD)
+        move_scales(0)
+        load_chunk(HEAD, HEAD, SECOND)
         move_scales(1)
         load_chunk(2 * HEAD, M - 2 * HEAD)
 
-        grouped_head0 = tile("grouped_head0", [P, PACK * HEAD], BF16)
-        hinge = tile("hinge", [P, PACK * P], BF16, HINGE)
-        grouped11 = tile("grouped11", [P, PACK * P], BF16)
-        group(nc.scalar.copy, grouped_head0[:], head0[:])
-        group(nc.scalar.copy, hinge[:], raws[0, 1])
-        group(nc.scalar.copy, grouped11[:], raws[1, 1])
+        first = {m: tile(f"grouped{m}", [P, PASSES, PACK * P], BF16, None if m else FIRST) for m in (0, 1)}
+        for a in range(PASSES):
+            for m in (0, 1):
+                group(nc.scalar.copy, first[m][:, a, :], raws[m, a])
         gather_words(0)
-        part(0)
         gather_words(1)
-        quantize(grouped_head0[:], [(0, 0), (1, 0)])
-        quantize(hinge[:], [(0, 1)])
-        product(0, 0)
-        part(1, BELOW)
-        quantize(grouped11[:], [(1, 1)])
-        product(0, 1)
-        store(0, 1, 0, 2)
-        product(1, 0)
-        product(1, 1)
-        store(1, 2, 0, 2)
-
-        second = {2: group_tile(2, ABOVE), 3: group_tile(3)}
-        for m in (2, 3):
-            quantize_tile(m, second[m])
-            product(m, 0)
-            product(m, 1)
+        part(0)
+        quantize_tile(0, first[0])
+        part(1, FIRST)
+        quantize_tile(1, first[1], THIRD)
+        for m in (0, 1):
+            products((m, 0))
+            products((m, 1))
             store(m, m + 1, 0, 2)
-        for s in (2, 3):
-            gather_words(s, ABOVE)
-            part(s)
-        for m in range(3):
-            product(m, 2)
-            store(m, m + 1, 2, 3)
-        product(3, 2)
-        product(3, 3)
-        store(3, 4, 2, SLICES)
-        for m in range(3):
-            product(m, 3)
-            store(m, m + 1, 3, SLICES)
+
+        second = {m: tile(f"grouped{m}", [P, PASSES, PACK * P], BF16) for m in (2, 3)}
+        for a in range(PASSES):
+            for m in (2, 3):
+                group(nc.vector.tensor_copy, second[m][:, a, :], raws[m, a])
+        quantize_tile(2, second[2])
+        gather_words(2, SECOND)
+        quantize_tile(3, second[3], THIRD + LAST)
+        part(2)
+        gather_words(3, SECOND + SLICE)
+        part(3)
+        for m in (2, 3):
+            products((m, 0))
+            products((m, 1))
+            store(m, m + 1, 0, 2)
+        for m in (0, 2):
+            products((m, 2))
+            products((m + 1, 2))
+            store(m, m + 2, 2, 3)
+        for m in (0, 2):
+            corner = tile(f"corner{m}", [P, 2, N], F32, THIRD + LAST * (m // 2))
+            products((m, 3), (m + 1, 3), into=corner)
+            rows = out[P * m : P * (m + 2), 3 * N : S].rearrange("(m p) c -> p m c", p=P)
+            nc.sync.dma_start(out=rows, in_=corner[:])
 
         for m in range(4, M_TILES):
-            quantize_tile(m, group_tile(m))
-        for m in range(4, M_TILES - 1):
-            for s in range(0, SLICES, 2):
-                product(m, s)
-                product(m, s + 1)
-                store(m, m + 1, s, s + 2)
-        m = M_TILES - 1
-        product(m, 0)
-        product(m, 1)
-        store(m, m + 1, 0, 2)
-        product(m, 2)
-        store(m, m + 1, 2, 3)
-        product(m, 3)
-        store(m, m + 1, 3, SLICES, nc.scalar)
+            quantize_tile(m, group_tile(m), THIRD + LAST * (m - 2))
+        for m in range(4, M_TILES):
+            products((m, 0))
+            store(m, m + 1, 0, 1)
+            rest = tile(f"rest{m}", [P, 3, N], F32, THIRD + LAST * (m - 2))
+            products((m, 1), (m, 2), (m, 3), into=rest)
+            rows = out[P * m : P * (m + 1), N:S].rearrange("p (s c) -> p s c", c=N)
+            if m < M_TILES - 1:
+                nc.sync.dma_start(out=rows[:, 0:2, :], in_=rest[:, 0:2, :])
+                nc.sync.dma_start(out=rows[:, 2, :], in_=rest[:, 2, :])
+        nc.sync.dma_start(out=rows[:, 0, :], in_=rest[:, 0, :])
+        nc.sync.dma_start(out=rows[:, 1, :], in_=rest[:, 1, :])
+        nc.scalar.dma_start(out=rows[:, 2, :], in_=rest[:, 2, :])

@@ -32,8 +32,7 @@ SLICE = 4 * N
 RAW = 4 * PACK * HEAD
 FIRST = 0
 THIRD = FIRST + SLICE
-LAST = 3 * 4 * N
-SECOND = THIRD + 6 * LAST
+SECOND = THIRD + 20 * SLICE
 
 
 def tile_list_tab4_gelu_kernel(tc, tab, w, b, offs, out):
@@ -55,7 +54,7 @@ def tile_list_tab4_gelu_kernel(tc, tab, w, b, offs, out):
         b_rows = tile("b_rows", [P, P], F32)
         b_cols = tile("b_cols", [P, M_TILES], F32)
         identity = tile("identity", [P, P], F32)
-        results = tile("results", [P, M_TILES, S], F32)
+        results = tile("results", [P, 4, S], F32)
         raws, codes, code_scales, picked_words, parted, picked_scales = {}, {}, {}, {}, {}, {}
 
         def load_w(raw, a, c0):
@@ -118,20 +117,23 @@ def tile_list_tab4_gelu_kernel(tc, tab, w, b, offs, out):
                 picked_words[s][:].bitcast(U16).rearrange("p (n a) -> p a n", a=PASSES),
             )
 
+        def one_pass(acc, m, s, a, start):
+            r, j0 = divmod(N * s, RUN)
+            nc.tensor.matmul_mx(
+                out=acc[:],
+                lhsT=codes[m, a].bitcast(E4M3),
+                lhsT_scale=code_scales[m, a],
+                rhs=parted[s][:, a, :].bitcast(E2M1),
+                rhs_scale=scales[r][:, RUN * a + j0 : RUN * a + j0 + N],
+                start=start,
+                stop=not start,
+            )
+
         def products(*pieces, into=None):
             banks = [psum.tile([P, N], F32, name="acc", tag="acc") for piece in pieces]
             for a in range(PASSES):
                 for (m, s), acc in zip(pieces, banks):
-                    r, j0 = divmod(N * s, RUN)
-                    nc.tensor.matmul_mx(
-                        out=acc[:],
-                        lhsT=codes[m, a].bitcast(E4M3),
-                        lhsT_scale=code_scales[m, a],
-                        rhs=parted[s][:, a, :].bitcast(E2M1),
-                        rhs_scale=scales[r][:, RUN * a + j0 : RUN * a + j0 + N],
-                        start=(a == 0),
-                        stop=(a == PASSES - 1),
-                    )
+                    one_pass(acc, m, s, a, a == 0)
             for j, ((m, s), acc) in enumerate(zip(pieces, banks)):
                 dst = results[:, m, N * s : N * (s + 1)] if into is None else into[:, j, :]
                 nc.scalar.activation(dst, acc[:], GELU, bias=b_cols[:, m : m + 1])
@@ -176,7 +178,7 @@ def tile_list_tab4_gelu_kernel(tc, tab, w, b, offs, out):
         part(0)
         quantize_tile(0, first[0])
         part(1, FIRST)
-        quantize_tile(1, first[1], THIRD)
+        quantize_tile(1, first[1])
         for m in (0, 1):
             products((m, 0))
             products((m, 1))
@@ -186,9 +188,9 @@ def tile_list_tab4_gelu_kernel(tc, tab, w, b, offs, out):
         for a in range(PASSES):
             for m in (2, 3):
                 group(nc.vector.tensor_copy, second[m][:, a, :], raws[m, a])
-        quantize_tile(2, second[2])
+        quantize_tile(2, second[2], THIRD)
         gather_words(2, SECOND)
-        quantize_tile(3, second[3], THIRD + LAST)
+        quantize_tile(3, second[3], THIRD + 2 * SLICE)
         part(2)
         gather_words(3, SECOND + SLICE)
         part(3)
@@ -196,27 +198,32 @@ def tile_list_tab4_gelu_kernel(tc, tab, w, b, offs, out):
             products((m, 0))
             products((m, 1))
             store(m, m + 1, 0, 2)
-        for m in (0, 2):
-            products((m, 2))
-            products((m + 1, 2))
-            store(m, m + 2, 2, 3)
-        for m in (0, 2):
-            corner = tile(f"corner{m}", [P, 2, N], F32, THIRD + LAST * (m // 2))
-            products((m, 3), (m + 1, 3), into=corner)
-            rows = out[P * m : P * (m + 2), 3 * N : S].rearrange("(m p) c -> p m c", p=P)
-            nc.sync.dma_start(out=rows, in_=corner[:])
+        for s in (2, 3):
+            for m in (0, 1):
+                products((m, s))
+        for m in (0, 1):
+            store(m, m + 1, 2, 4)
+        for m in (2, 3):
+            half = tile(f"half{m}", [P, 2, N], F32, THIRD + 2 * SLICE * (m - 2))
+            products((m, 2), (m, 3), into=half)
+            nc.sync.dma_start(out=out[P * m : P * (m + 1), 2 * N : S], in_=half[:].rearrange("p s c -> p (s c)"))
 
+        place = {(m, a): THIRD + 2 * SLICE * (2 * (m - 3) + a) for m in range(4, M_TILES) for a in range(PASSES)}
         for m in range(4, M_TILES):
-            quantize_tile(m, group_tile(m), THIRD + LAST * (m - 2))
+            grouped = group_tile(m)
+            for a in range(PASSES):
+                quantize(grouped[:, a, :], [(m, a)], place[m, a])
         for m in range(4, M_TILES):
-            products((m, 0))
-            store(m, m + 1, 0, 1)
-            rest = tile(f"rest{m}", [P, 3, N], F32, THIRD + LAST * (m - 2))
-            products((m, 1), (m, 2), (m, 3), into=rest)
-            rows = out[P * m : P * (m + 1), N:S].rearrange("p (s c) -> p s c", c=N)
-            if m < M_TILES - 1:
-                nc.sync.dma_start(out=rows[:, 0:2, :], in_=rest[:, 0:2, :])
-                nc.sync.dma_start(out=rows[:, 2, :], in_=rest[:, 2, :])
-        nc.sync.dma_start(out=rows[:, 0, :], in_=rest[:, 0, :])
-        nc.sync.dma_start(out=rows[:, 1, :], in_=rest[:, 1, :])
-        nc.scalar.dma_start(out=rows[:, 2, :], in_=rest[:, 2, :])
+            banks = {s: psum.tile([P, N], F32, name="acc", tag="acc") for s in (2, 3, 0, 1)}
+            for pair, a, start in (((2, 3), 0, True), ((0, 1), 1, True), ((0, 1), 0, False), ((2, 3), 1, False)):
+                for s in pair:
+                    one_pass(banks[s], m, s, a, start)
+            for h in range(2):
+                half = tile(f"half{m}{h}", [P, 2, N], F32, place[m, h])
+                for j in range(2):
+                    nc.scalar.activation(half[:, j, :], banks[2 * h + j][:], GELU, bias=b_cols[:, m : m + 1])
+                rows = out[P * m : P * (m + 1), 2 * N * h : 2 * N * (h + 1)]
+                if (m, h) != (M_TILES - 1, 1):
+                    nc.sync.dma_start(out=rows, in_=half[:].rearrange("p s c -> p (s c)"))
+        nc.sync.dma_start(out=rows[:, 0:N], in_=half[:, 0, :])
+        nc.scalar.dma_start(out=rows[:, N : 2 * N], in_=half[:, 1, :])

@@ -30,9 +30,9 @@ ROWS0 = P - QUAD
 
 SLICE = 4 * N
 RAW = 4 * PACK * HEAD
-FIRST = 0
-THIRD = FIRST + SLICE
-SECOND = THIRD + 20 * SLICE
+HEAD0 = 0
+HEAD1 = RAW
+SECOND = 2 * RAW
 
 
 def tile_list_tab4_gelu_kernel(tc, tab, w, b, offs, out):
@@ -54,7 +54,7 @@ def tile_list_tab4_gelu_kernel(tc, tab, w, b, offs, out):
         b_rows = tile("b_rows", [P, P], F32)
         b_cols = tile("b_cols", [P, M_TILES], F32)
         identity = tile("identity", [P, P], F32)
-        results = tile("results", [P, 4, S], F32)
+        results = tile("results", [P, M_TILES, S], F32)
         raws, codes, code_scales, picked_words, parted, picked_scales = {}, {}, {}, {}, {}, {}
 
         def load_w(raw, a, c0):
@@ -109,6 +109,19 @@ def tile_list_tab4_gelu_kernel(tc, tab, w, b, offs, out):
             cols = slice(s * N // 16, (s + 1) * N // 16)
             nc.vector.tensor_copy(picked_words[s][:].bitcast(U32), words[:].bitcast(U32).indirect(offsets[:, cols]))
 
+        def gather_half(s, h, offset=None):
+            picked_words[s, h] = tile(f"picked_words{s}{h}", [P, N // 2], I32, offset)
+            cols = slice((2 * s + h) * N // 32, (2 * s + h + 1) * N // 32)
+            nc.vector.tensor_copy(picked_words[s, h][:].bitcast(U32), words[:].bitcast(U32).indirect(offsets[:, cols]))
+
+        def part_halves(s, offset=None):
+            parted[s] = tile(f"parted{s}", [P, PASSES, 2 * N], U8, offset)
+            for h in range(2):
+                nc.vector.tensor_copy(
+                    parted[s][:, :, N * h : N * (h + 1)].bitcast(U16),
+                    picked_words[s, h][:].bitcast(U16).rearrange("p (n a) -> p a n", a=PASSES),
+                )
+
         def part(s, offset=None):
             parted[s] = tile(f"parted{s}", [P, PASSES, 2 * N], U8, offset)
             halves = parted[s][:].rearrange("p a c -> p (a c)").bitcast(U16)
@@ -149,7 +162,7 @@ def tile_list_tab4_gelu_kernel(tc, tab, w, b, offs, out):
             in_=tab[0, 4 * P * T :].rearrange("(a g t) -> g a t", a=PASSES, t=T).bitcast(I32),
         )
         nc.sync.dma_start(out=words[:], in_=tab[0, 0 : 4 * P * T].rearrange("(p c) -> p c", p=P).bitcast(I32))
-        head0 = tile("head0", [P, PACK, HEAD], F32)
+        head0 = tile("head0", [P, PACK, HEAD], F32, HEAD0)
         load_w(head0, 0, 0)
 
         nc.scalar.dma_start(out=b_rows[P - M_TILES : P, :], in_=b.rearrange("(m p) -> m p", p=P))
@@ -163,24 +176,28 @@ def tile_list_tab4_gelu_kernel(tc, tab, w, b, offs, out):
 
         for r in range(S // RUN):
             gather_scales(r)
-        load_w(tile("head1", [P, PACK, HEAD], F32), 1, 0)
+        load_w(tile("head1", [P, PACK, HEAD], F32, HEAD1), 1, 0)
         move_scales(0)
         load_chunk(HEAD, HEAD, SECOND)
         move_scales(1)
         load_chunk(2 * HEAD, M - 2 * HEAD)
 
-        first = {m: tile(f"grouped{m}", [P, PASSES, PACK * P], BF16, None if m else FIRST) for m in (0, 1)}
-        for a in range(PASSES):
-            for m in (0, 1):
-                group(nc.scalar.copy, first[m][:, a, :], raws[m, a])
-        gather_words(0)
-        gather_words(1)
-        part(0)
-        quantize_tile(0, first[0])
-        part(1, FIRST)
-        quantize_tile(1, first[1])
+        early = tile("early", [P, 2, PACK * P], BF16)
+        late = {m: tile(f"late{m}", [P, PACK * P], BF16) for m in (0, 1)}
         for m in (0, 1):
-            products((m, 0))
+            group(nc.scalar.copy, early[:, m, :], raws[m, 0])
+        for m in (0, 1):
+            group(nc.scalar.copy, late[m][:], raws[m, 1])
+        gather_words(0)
+        gather_half(1, 0)
+        part(0)
+        quantize(early[:].rearrange("p a c -> p (a c)"), [(0, 0), (1, 0)])
+        gather_half(1, 1, HEAD0)
+        quantize(late[0][:], [(0, 1)])
+        quantize(late[1][:], [(1, 1)])
+        part_halves(1, HEAD1)
+        products((0, 0), (1, 0))
+        for m in (0, 1):
             products((m, 1))
             store(m, m + 1, 0, 2)
 
@@ -188,12 +205,12 @@ def tile_list_tab4_gelu_kernel(tc, tab, w, b, offs, out):
         for a in range(PASSES):
             for m in (2, 3):
                 group(nc.vector.tensor_copy, second[m][:, a, :], raws[m, a])
-        quantize_tile(2, second[2], THIRD)
-        gather_words(2, SECOND)
-        quantize_tile(3, second[3], THIRD + 2 * SLICE)
-        part(2)
-        gather_words(3, SECOND + SLICE)
-        part(3)
+        for m in (2, 3):
+            quantize_tile(m, second[m])
+        for s in (2, 3):
+            for h in range(2):
+                gather_half(s, h, SECOND + h * SLICE // 2)
+            part_halves(s)
         for m in (2, 3):
             products((m, 0))
             products((m, 1))
@@ -204,26 +221,27 @@ def tile_list_tab4_gelu_kernel(tc, tab, w, b, offs, out):
         for m in (0, 1):
             store(m, m + 1, 2, 4)
         for m in (2, 3):
-            half = tile(f"half{m}", [P, 2, N], F32, THIRD + 2 * SLICE * (m - 2))
-            products((m, 2), (m, 3), into=half)
-            nc.sync.dma_start(out=out[P * m : P * (m + 1), 2 * N : S], in_=half[:].rearrange("p s c -> p (s c)"))
+            products((m, 2))
+            products((m, 3))
+            store(m, m + 1, 2, 4)
 
-        place = {(m, a): THIRD + 2 * SLICE * (2 * (m - 3) + a) for m in range(4, M_TILES) for a in range(PASSES)}
         for m in range(4, M_TILES):
-            grouped = group_tile(m)
-            for a in range(PASSES):
-                quantize(grouped[:, a, :], [(m, a)], place[m, a])
-        for m in range(4, M_TILES):
-            banks = {s: psum.tile([P, N], F32, name="acc", tag="acc") for s in (2, 3, 0, 1)}
-            for pair, a, start in (((2, 3), 0, True), ((0, 1), 1, True), ((0, 1), 0, False), ((2, 3), 1, False)):
-                for s in pair:
-                    one_pass(banks[s], m, s, a, start)
+            quantize_tile(m, group_tile(m))
+        for m in range(4, M_TILES - 1):
             for h in range(2):
-                half = tile(f"half{m}{h}", [P, 2, N], F32, place[m, h])
-                for j in range(2):
-                    nc.scalar.activation(half[:, j, :], banks[2 * h + j][:], GELU, bias=b_cols[:, m : m + 1])
-                rows = out[P * m : P * (m + 1), 2 * N * h : 2 * N * (h + 1)]
-                if (m, h) != (M_TILES - 1, 1):
-                    nc.sync.dma_start(out=rows, in_=half[:].rearrange("p s c -> p (s c)"))
-        nc.sync.dma_start(out=rows[:, 0:N], in_=half[:, 0, :])
-        nc.scalar.dma_start(out=rows[:, N : 2 * N], in_=half[:, 1, :])
+                products((m, 2 * h))
+                products((m, 2 * h + 1))
+                store(m, m + 1, 2 * h, 2 * h + 2)
+        m = M_TILES - 1
+        products((m, 0))
+        products((m, 1))
+        store(m, m + 1, 0, 2)
+        products((m, 2))
+        store(m, m + 1, 2, 3)
+        acc = psum.tile([P, N], F32, name="acc", tag="acc")
+        for a in range(PASSES):
+            one_pass(acc, m, 3, a, a == 0)
+        for h, queue in enumerate((nc.sync, nc.scalar)):
+            cols = slice(S - N + h * N // 2, S - N + (h + 1) * N // 2)
+            nc.scalar.activation(results[:, m, cols], acc[:, h * N // 2 : (h + 1) * N // 2], GELU, bias=b_cols[:, m : m + 1])
+            queue.dma_start(out=out[P * m : P * (m + 1), cols], in_=results[:, m, cols])

@@ -24,7 +24,7 @@ M_TILES = M // P
 
 N = 512
 SLICES = S // N
-RUN = 1024
+RUNS = ((0, 1), (1, 2), (2, 4))
 HEAD = 256
 ROWS0 = P - QUAD
 
@@ -50,7 +50,7 @@ def tile_list_tab4_gelu_kernel(tc, tab, w, b, offs, out):
         offsets = keep.tile([P, S // 16], U16, name="offsets")
         words = tile("words", [P, T], I32)
         table_scales = tile("table_scales", [P, T], U8)
-        scales = [tile(f"scales{r}", [P, PASSES * RUN], U8) for r in range(S // RUN)]
+        scales = [tile(f"scales{r}", [P, PASSES * N * (s1 - s0)], U8) for r, (s0, s1) in enumerate(RUNS)]
         b_rows = tile("b_rows", [P, P], F32)
         b_cols = tile("b_cols", [P, M_TILES], F32)
         identity = tile("identity", [P, P], F32)
@@ -69,8 +69,9 @@ def tile_list_tab4_gelu_kernel(tc, tab, w, b, offs, out):
                 load_w(tile(f"raw{c0}_{a}", [P, PACK, width], F32, offset if a else None), a, c0)
 
         def gather_scales(r):
-            picked_scales[r] = tile(f"picked_scales{r}", [P, RUN], U8)
-            cols = slice(r * RUN // 16, (r + 1) * RUN // 16)
+            s0, s1 = RUNS[r]
+            picked_scales[r] = tile(f"picked_scales{r}", [P, N * (s1 - s0)], U8)
+            cols = slice(s0 * N // 16, s1 * N // 16)
             nc.vector.tensor_copy(picked_scales[r][:], table_scales[:].indirect(offsets[:, cols]))
 
         def move_scales(r):
@@ -131,13 +132,15 @@ def tile_list_tab4_gelu_kernel(tc, tab, w, b, offs, out):
             )
 
         def one_pass(acc, m, s, a, start):
-            r, j0 = divmod(N * s, RUN)
+            r = min(s, 2)
+            s0, s1 = RUNS[r]
+            j0 = N * ((s1 - s0) * a + s - s0)
             nc.tensor.matmul_mx(
                 out=acc[:],
                 lhsT=codes[m, a].bitcast(E4M3),
                 lhsT_scale=code_scales[m, a],
                 rhs=parted[s][:, a, :].bitcast(E2M1),
-                rhs_scale=scales[r][:, RUN * a + j0 : RUN * a + j0 + N],
+                rhs_scale=scales[r][:, j0 : j0 + N],
                 start=start,
                 stop=not start,
             )
@@ -162,24 +165,24 @@ def tile_list_tab4_gelu_kernel(tc, tab, w, b, offs, out):
             in_=tab[0, 4 * P * T :].rearrange("(a g t) -> g a t", a=PASSES, t=T).bitcast(I32),
         )
         nc.sync.dma_start(out=words[:], in_=tab[0, 0 : 4 * P * T].rearrange("(p c) -> p c", p=P).bitcast(I32))
-        head0 = tile("head0", [P, PACK, HEAD], F32, HEAD0)
-        load_w(head0, 0, 0)
 
         nc.scalar.dma_start(out=b_rows[P - M_TILES : P, :], in_=b.rearrange("(m p) -> m p", p=P))
         make_identity(nc, identity[:])
         nc.scalar.activation(b_rows[0 : P - M_TILES, :], identity[0 : P - M_TILES, :], GELU, scale=0.0)
-        for r in range(S // RUN):
+        for r in range(len(RUNS)):
             nc.gpsimd.memset(scales[r][:].bitcast(I32), 0)
         b_bank = psum.tile([P, N], F32, name="b_bank", tag="acc")
         nc.tensor.transpose(b_bank[:, 0:P], b_rows[:], identity[:])
         nc.scalar.copy(b_cols[:], b_bank[:, P - M_TILES : P])
 
-        for r in range(S // RUN):
+        for r in range(len(RUNS)):
             gather_scales(r)
-        load_w(tile("head1", [P, PACK, HEAD], F32, HEAD1), 1, 0)
         move_scales(0)
-        load_chunk(HEAD, HEAD, SECOND)
+        load_w(tile("head0", [P, PACK, HEAD], F32, HEAD0), 0, 0)
+        load_w(tile("head1", [P, PACK, HEAD], F32, HEAD1), 1, 0)
         move_scales(1)
+        load_chunk(HEAD, HEAD, SECOND)
+        move_scales(2)
         load_chunk(2 * HEAD, M - 2 * HEAD)
 
         early = tile("early", [P, 2, PACK * P], BF16)
@@ -216,14 +219,10 @@ def tile_list_tab4_gelu_kernel(tc, tab, w, b, offs, out):
             products((m, 1))
             store(m, m + 1, 0, 2)
         for s in (2, 3):
-            for m in (0, 1):
+            for m in (0, 2):
                 products((m, s))
-        for m in (0, 1):
-            store(m, m + 1, 2, 4)
-        for m in (2, 3):
-            products((m, 2))
-            products((m, 3))
-            store(m, m + 1, 2, 4)
+                products((m + 1, s))
+                store(m, m + 2, s, s + 1)
 
         for m in range(4, M_TILES):
             quantize_tile(m, group_tile(m))

@@ -32,6 +32,7 @@ SLICE = 4 * N
 RAW = 4 * PACK * HEAD
 HEAD0 = 0
 HEAD1 = RAW
+LAST = 3 * RAW
 SECOND = 2 * RAW
 
 
@@ -54,7 +55,7 @@ def tile_list_tab4_gelu_kernel(tc, tab, w, b, offs, out):
         b_rows = tile("b_rows", [P, P], F32)
         b_cols = tile("b_cols", [P, M_TILES], F32)
         identity = tile("identity", [P, P], F32)
-        results = tile("results", [P, M_TILES, S], F32)
+        results = tile("results", [P, 4, S], F32)
         raws, codes, code_scales, picked_words, parted, picked_scales = {}, {}, {}, {}, {}, {}
 
         def load_w(raw, a, c0):
@@ -131,14 +132,15 @@ def tile_list_tab4_gelu_kernel(tc, tab, w, b, offs, out):
                 picked_words[s][:].bitcast(U16).rearrange("p (n a) -> p a n", a=PASSES),
             )
 
-        def one_pass(acc, m, s, a, start):
+        def one_pass(acc, m, s, a, start, piece=None):
+            piece = a if piece is None else piece
             r = min(s, 2)
             s0, s1 = RUNS[r]
             j0 = N * ((s1 - s0) * a + s - s0)
             nc.tensor.matmul_mx(
                 out=acc[:],
-                lhsT=codes[m, a].bitcast(E4M3),
-                lhsT_scale=code_scales[m, a],
+                lhsT=codes[m, piece].bitcast(E4M3),
+                lhsT_scale=code_scales[m, piece],
                 rhs=parted[s][:, a, :].bitcast(E2M1),
                 rhs_scale=scales[r][:, j0 : j0 + N],
                 start=start,
@@ -177,24 +179,27 @@ def tile_list_tab4_gelu_kernel(tc, tab, w, b, offs, out):
 
         for r in range(len(RUNS)):
             gather_scales(r)
-        move_scales(0)
         load_w(tile("head0", [P, PACK, HEAD], F32, HEAD0), 0, 0)
+        move_scales(0)
         load_w(tile("head1", [P, PACK, HEAD], F32, HEAD1), 1, 0)
+        load_w(tile("second0", [P, PACK, HEAD], F32), 0, HEAD)
         move_scales(1)
-        load_chunk(HEAD, HEAD, SECOND)
+        load_w(tile("second1", [P, PACK, HEAD], F32, SECOND), 1, HEAD)
+        load_w(tile("third0", [P, PACK, 2 * HEAD], F32), 0, 2 * HEAD)
         move_scales(2)
-        load_chunk(2 * HEAD, M - 2 * HEAD)
+        load_w(tile("third1", [P, PACK, 2 * HEAD], F32), 1, 2 * HEAD)
 
-        early = tile("early", [P, 2, PACK * P], BF16)
+        early = {m: tile(f"early{m}", [P, PACK * P], BF16) for m in (0, 1)}
         late = {m: tile(f"late{m}", [P, PACK * P], BF16) for m in (0, 1)}
         for m in (0, 1):
-            group(nc.scalar.copy, early[:, m, :], raws[m, 0])
+            group(nc.scalar.copy, early[m][:], raws[m, 0])
         for m in (0, 1):
             group(nc.scalar.copy, late[m][:], raws[m, 1])
         gather_words(0)
         gather_half(1, 0)
         part(0)
-        quantize(early[:].rearrange("p a c -> p (a c)"), [(0, 0), (1, 0)])
+        for m in (0, 1):
+            quantize(early[m][:], [(m, 0)])
         gather_half(1, 1, HEAD0)
         quantize(late[0][:], [(0, 1)])
         quantize(late[1][:], [(1, 1)])
@@ -225,22 +230,23 @@ def tile_list_tab4_gelu_kernel(tc, tab, w, b, offs, out):
                 store(m, m + 2, s, s + 1)
 
         for m in range(4, M_TILES):
-            quantize_tile(m, group_tile(m))
-        for m in range(4, M_TILES - 1):
+            grouped = group_tile(m)
+            quantize(grouped[:, 0, :], [(m, 0)])
             for h in range(2):
-                products((m, 2 * h))
-                products((m, 2 * h + 1))
-                store(m, m + 1, 2 * h, 2 * h + 2)
-        m = M_TILES - 1
-        products((m, 0))
-        products((m, 1))
-        store(m, m + 1, 0, 2)
-        products((m, 2))
-        store(m, m + 1, 2, 3)
-        acc = psum.tile([P, N], F32, name="acc", tag="acc")
-        for a in range(PASSES):
-            one_pass(acc, m, 3, a, a == 0)
-        for h, queue in enumerate((nc.sync, nc.scalar)):
-            cols = slice(S - N + h * N // 2, S - N + (h + 1) * N // 2)
-            nc.scalar.activation(results[:, m, cols], acc[:, h * N // 2 : (h + 1) * N // 2], GELU, bias=b_cols[:, m : m + 1])
-            queue.dma_start(out=out[P * m : P * (m + 1), cols], in_=results[:, m, cols])
+                quantize(grouped[:, 1, :], [(m, 1 + h)], LAST + RAW * (2 * (m - 4) + h))
+        for m in range(4, M_TILES):
+            for h in range(2):
+                banks = [psum.tile([P, N], F32, name="acc", tag="acc") for j in range(2)]
+                for a in range(PASSES):
+                    for j in range(2):
+                        one_pass(banks[j], m, 2 * h + j, a, a == 0, a * (1 + h))
+                half = tile(f"half{m}{h}", [P, 2 * N], F32, LAST + RAW * (2 * (m - 4) + h))
+                rows = out[P * m : P * (m + 1), 2 * N * h : 2 * N * (h + 1)]
+                if (m, h) != (M_TILES - 1, 1):
+                    for j in range(2):
+                        nc.scalar.activation(half[:, N * j : N * (j + 1)], banks[j][:], GELU, bias=b_cols[:, m : m + 1])
+                    nc.sync.dma_start(out=rows, in_=half[:])
+        for j, c0, c1, queue in ((0, 0, N, nc.sync), (1, 0, N // 2, nc.sync), (1, N // 2, N, nc.scalar)):
+            cols = slice(N * j + c0, N * j + c1)
+            nc.scalar.activation(half[:, cols], banks[j][:, c0:c1], GELU, bias=b_cols[:, m : m + 1])
+            queue.dma_start(out=rows[:, cols], in_=half[:, cols])

@@ -26,6 +26,7 @@ N = 512
 SLICES = S // N
 RUNS = ((0, 1), (1, 2), (2, 4))
 HEAD = 256
+ALIGN = 256
 ROWS0 = P - QUAD
 
 SLICE = 4 * N
@@ -45,10 +46,10 @@ def tile_list_tab4_gelu_kernel(tc, tab, w, b, offs, out):
 
         def tile(name, shape, dtype, offset=None):
             if offset is None:
-                return keep.tile(shape, dtype, name=name, align_bytes=64)
-            return shared.tile(shape, dtype, name=name, offset=offset, align_bytes=64)
+                return keep.tile(shape, dtype, name=name, align_bytes=ALIGN)
+            return shared.tile(shape, dtype, name=name, offset=offset, align_bytes=ALIGN)
 
-        offsets = keep.tile([P, S // 16], U16, name="offsets")
+        offsets = keep.tile([P, S // 16], U16, name="offsets", align_bytes=ALIGN)
         words = tile("words", [P, T], I32)
         table_scales = tile("table_scales", [P, T], U8)
         scales = [tile(f"scales{r}", [P, PASSES * N * (s1 - s0)], U8) for r, (s0, s1) in enumerate(RUNS)]

@@ -21,20 +21,15 @@ QUAD = 32
 PACK = 4
 PASSES = K // (P * PACK)
 M_TILES = M // P
-
 N = 512
+HALF = N // 2
 SLICES = S // N
-RUNS = ((0, 1), (1, 2), (2, 4))
-HEAD = 256
 ALIGN = 256
 ROWS0 = P - QUAD
-
-SLICE = 4 * N
+RUNS = ((0, 2), (2, 4))
+HEAD = 256
 RAW = 4 * PACK * HEAD
-HEAD0 = 0
-HEAD1 = RAW
-LAST = 3 * RAW
-SECOND = 2 * RAW
+HEAD0, HEAD1, SECOND1 = 0, RAW, 2 * RAW + 1024
 
 
 def tile_list_tab4_gelu_kernel(tc, tab, w, b, offs, out):
@@ -56,19 +51,14 @@ def tile_list_tab4_gelu_kernel(tc, tab, w, b, offs, out):
         b_rows = tile("b_rows", [P, P], F32)
         b_cols = tile("b_cols", [P, M_TILES], F32)
         identity = tile("identity", [P, P], F32)
-        results = tile("results", [P, 4, S], F32)
-        raws, codes, code_scales, picked_words, parted, picked_scales = {}, {}, {}, {}, {}, {}
+        raws, grouped, codes, code_scales, picked_words, parted, picked_scales = {}, {}, {}, {}, {}, {}, {}
 
-        def load_w(raw, a, c0):
-            width = raw.shape[2]
+        def load_w(a, c0, width, offset=None):
+            raw = tile(f"raw{c0}_{a}", [P, PACK, width], F32, offset)
             rows = w[P * PACK * a : P * PACK * (a + 1), c0 : c0 + width].rearrange("(p i) c -> p i c", i=PACK)
             nc.sync.dma_start(out=raw[:], in_=rows)
             for j in range(width // P):
                 raws[c0 // P + j, a] = raw[:, :, P * j : P * (j + 1)]
-
-        def load_chunk(c0, width, offset=None):
-            for a in range(PASSES):
-                load_w(tile(f"raw{c0}_{a}", [P, PACK, width], F32, offset if a else None), a, c0)
 
         def gather_scales(r):
             s0, s1 = RUNS[r]
@@ -76,56 +66,63 @@ def tile_list_tab4_gelu_kernel(tc, tab, w, b, offs, out):
             cols = slice(s0 * N // 16, s1 * N // 16)
             nc.vector.tensor_copy(picked_scales[r][:], table_scales[:].indirect(offsets[:, cols]))
 
-        def move_scales(r):
+        def move_scales(r, queue=nc.sync):
             for q in (0, 2, 1, 3):
-                nc.sync.dma_start(
+                queue.dma_start(
                     out=scales[r][QUAD * q : QUAD * q + 4, :].bitcast(I32),
                     in_=picked_scales[r][ROWS0 + 8 * q : ROWS0 + 8 * (q + 1), :].bitcast(I32),
                 )
 
-        def group(copy, dst, src):
+        def group(copy, m, a, offset=None):
+            grouped[m, a] = tile(f"grouped{m}_{a}", [P, PACK * P], BF16, offset)
             copy(
-                dst.rearrange("p (c j i) -> p c i j", j=PACK, i=PACK),
-                src.rearrange("p i (c j) -> p c i j", j=PACK),
+                grouped[m, a][:].rearrange("p (c j i) -> p c i j", j=PACK, i=PACK),
+                raws[m, a].rearrange("p i (c j) -> p c i j", j=PACK),
+            )
+
+        def group_both(m, offset=None):
+            both = tile(f"both{m}", [P, PASSES, PACK * P], BF16, offset)
+            grouped[m] = both
+            for a in range(PASSES):
+                grouped[m, a] = both[:, a, :]
+
+        def group_into(copy, m, a):
+            copy(
+                grouped[m, a].rearrange("p (c j i) -> p c i j", j=PACK, i=PACK),
+                raws[m, a].rearrange("p i (c j) -> p c i j", j=PACK),
             )
 
         def quantize(src, pieces, offset=None):
             m, a = pieces[0]
-            piece_codes = tile(f"codes{m}{a}", [P, P * len(pieces)], U32, offset)
-            piece_scales = tile(f"code_scales{m}{a}", [P, P * len(pieces)], U8)
+            piece_codes = tile(f"codes{m}_{a}", [P, P * len(pieces)], U32, offset)
+            piece_scales = tile(f"code_scales{m}_{a}", [P, P * len(pieces)], U8)
             nc.vector.quantize_mx(out=piece_codes[:].bitcast(E4M3), scales=piece_scales[:], in_=src)
             for j, piece in enumerate(pieces):
                 codes[piece] = piece_codes[:, P * j : P * (j + 1)]
                 code_scales[piece] = piece_scales[:, P * j : P * (j + 1)]
 
-        def group_tile(m, offset=None):
-            grouped = tile(f"grouped{m}", [P, PASSES, PACK * P], BF16, offset)
-            for a in range(PASSES):
-                group(nc.vector.tensor_copy, grouped[:, a, :], raws[m, a])
-            return grouped
+        def quantize_both(m):
+            quantize(grouped[m][:].rearrange("p a c -> p (a c)"), [(m, a) for a in range(PASSES)])
 
-        def quantize_tile(m, grouped, offset=None):
-            quantize(grouped[:].rearrange("p a c -> p (a c)"), [(m, a) for a in range(PASSES)], offset)
+        def gather_half(s, h, offset=None):
+            picked_words[s, h] = tile(f"picked_words{s}_{h}", [P, HALF], I32, offset)
+            cols = slice((2 * s + h) * HALF // 16, (2 * s + h + 1) * HALF // 16)
+            nc.vector.tensor_copy(picked_words[s, h][:].bitcast(U32), words[:].bitcast(U32).indirect(offsets[:, cols]))
 
-        def gather_words(s, offset=None):
+        def part_half(s, h, offset=None):
+            if s not in parted:
+                parted[s] = tile(f"parted{s}", [P, PASSES, 2 * N], U8, offset)
+            nc.vector.tensor_copy(
+                parted[s][:, :, N * h : N * (h + 1)].bitcast(U16),
+                picked_words[s, h][:].bitcast(U16).rearrange("p (n a) -> p a n", a=PASSES),
+            )
+
+        def gather_whole(s, offset=None):
             picked_words[s] = tile(f"picked_words{s}", [P, N], I32, offset)
             cols = slice(s * N // 16, (s + 1) * N // 16)
             nc.vector.tensor_copy(picked_words[s][:].bitcast(U32), words[:].bitcast(U32).indirect(offsets[:, cols]))
 
-        def gather_half(s, h, offset=None):
-            picked_words[s, h] = tile(f"picked_words{s}{h}", [P, N // 2], I32, offset)
-            cols = slice((2 * s + h) * N // 32, (2 * s + h + 1) * N // 32)
-            nc.vector.tensor_copy(picked_words[s, h][:].bitcast(U32), words[:].bitcast(U32).indirect(offsets[:, cols]))
-
-        def part_halves(s, offset=None):
-            parted[s] = tile(f"parted{s}", [P, PASSES, 2 * N], U8, offset)
-            for h in range(2):
-                nc.vector.tensor_copy(
-                    parted[s][:, :, N * h : N * (h + 1)].bitcast(U16),
-                    picked_words[s, h][:].bitcast(U16).rearrange("p (n a) -> p a n", a=PASSES),
-                )
-
-        def part(s, offset=None):
+        def part_whole(s, offset=None):
             parted[s] = tile(f"parted{s}", [P, PASSES, 2 * N], U8, offset)
             halves = parted[s][:].rearrange("p a c -> p (a c)").bitcast(U16)
             nc.vector.tensor_copy(
@@ -133,9 +130,9 @@ def tile_list_tab4_gelu_kernel(tc, tab, w, b, offs, out):
                 picked_words[s][:].bitcast(U16).rearrange("p (n a) -> p a n", a=PASSES),
             )
 
-        def one_pass(acc, m, s, a, start, piece=None):
+        def one_pass(acc, m, s, a, piece=None):
             piece = a if piece is None else piece
-            r = min(s, 2)
+            r = [s0 <= s < s1 for s0, s1 in RUNS].index(True)
             s0, s1 = RUNS[r]
             j0 = N * ((s1 - s0) * a + s - s0)
             nc.tensor.matmul_mx(
@@ -144,110 +141,124 @@ def tile_list_tab4_gelu_kernel(tc, tab, w, b, offs, out):
                 lhsT_scale=code_scales[m, piece],
                 rhs=parted[s][:, a, :].bitcast(E2M1),
                 rhs_scale=scales[r][:, j0 : j0 + N],
-                start=start,
-                stop=not start,
+                start=a == 0,
+                stop=a == PASSES - 1,
             )
 
-        def products(*pieces, into=None):
-            banks = [psum.tile([P, N], F32, name="acc", tag="acc") for piece in pieces]
+        def bank():
+            return psum.tile([P, N], F32, name="acc", tag="acc")
+
+        def products(*pieces):
+            banks = [bank() for piece in pieces]
             for a in range(PASSES):
                 for (m, s), acc in zip(pieces, banks):
-                    one_pass(acc, m, s, a, a == 0)
-            for j, ((m, s), acc) in enumerate(zip(pieces, banks)):
-                dst = results[:, m, N * s : N * (s + 1)] if into is None else into[:, j, :]
-                nc.scalar.activation(dst, acc[:], GELU, bias=b_cols[:, m : m + 1])
+                    one_pass(acc, m, s, a)
+            for (m, s), acc in zip(pieces, banks):
+                nc.scalar.activation(results[m][:, N * s : N * (s + 1)], acc[:], GELU, bias=b_cols[:, m : m + 1])
 
-        def store(m0, m1, s0, s1, queue=nc.sync):
-            rows = out[P * m0 : P * m1, N * s0 : N * s1].rearrange("(m p) c -> p m c", p=P)
-            queue.dma_start(out=rows, in_=results[:, m0:m1, N * s0 : N * s1])
+        def store(m, s0, s1, queue=nc.sync):
+            queue.dma_start(out=out[P * m : P * (m + 1), N * s0 : N * s1], in_=results[m][:, N * s0 : N * s1])
 
-        nc.vector.memset(table_scales[0:ROWS0, :].bitcast(I32), 0)
-        nc.sync.dma_start(offsets[:], offs)
-        nc.sync.dma_start(
-            out=table_scales[ROWS0:P, :].bitcast(I32),
-            in_=tab[0, 4 * P * T :].rearrange("(a g t) -> g a t", a=PASSES, t=T).bitcast(I32),
-        )
-        nc.sync.dma_start(out=words[:], in_=tab[0, 0 : 4 * P * T].rearrange("(p c) -> p c", p=P).bitcast(I32))
+        def store_pair(m, s):
+            rows = out[P * m : P * (m + 2), N * s : N * (s + 1)].rearrange("(m p) c -> p m c", p=P)
+            nc.sync.dma_start(out=rows, in_=first[:, m : m + 2, N * s : N * (s + 1)])
 
-        nc.scalar.dma_start(out=b_rows[P - M_TILES : P, :], in_=b.rearrange("(m p) -> m p", p=P))
-        make_identity(nc, identity[:])
-        nc.scalar.activation(b_rows[0 : P - M_TILES, :], identity[0 : P - M_TILES, :], GELU, scale=0.0)
-        for r in range(len(RUNS)):
-            nc.gpsimd.memset(scales[r][:].bitcast(I32), 0)
-        b_bank = psum.tile([P, N], F32, name="b_bank", tag="acc")
-        nc.tensor.transpose(b_bank[:, 0:P], b_rows[:], identity[:])
-        nc.scalar.copy(b_cols[:], b_bank[:, P - M_TILES : P])
+        def head():
+            nc.vector.memset(table_scales[0:ROWS0, :].bitcast(I32), 0)
+            nc.sync.dma_start(offsets[:], offs)
+            nc.sync.dma_start(
+                out=table_scales[ROWS0:P, :].bitcast(I32),
+                in_=tab[0, 4 * P * T :].rearrange("(a g t) -> g a t", a=PASSES, t=T).bitcast(I32),
+            )
+            nc.sync.dma_start(out=words[:], in_=tab[0, 0 : 4 * P * T].rearrange("(p c) -> p c", p=P).bitcast(I32))
+            nc.scalar.dma_start(out=b_rows[P - M_TILES : P, :], in_=b.rearrange("(m p) -> m p", p=P))
+            make_identity(nc, identity[:])
+            nc.scalar.activation(b_rows[0 : P - M_TILES, :], identity[0 : P - M_TILES, :], GELU, scale=0.0)
+            for r in range(len(RUNS)):
+                nc.gpsimd.memset(scales[r][:].bitcast(I32), 0)
+            b_bank = bank()
+            nc.tensor.transpose(b_bank[:, 0:P], b_rows[:], identity[:])
+            nc.scalar.copy(b_cols[:], b_bank[:, P - M_TILES : P])
+            for r in range(len(RUNS)):
+                gather_scales(r)
 
-        for r in range(len(RUNS)):
-            gather_scales(r)
-        load_w(tile("head0", [P, PACK, HEAD], F32, HEAD0), 0, 0)
+        first = tile("first", [P, 4, S], F32)
+        results = {m: first[:, m, :] for m in range(4)}
+        head()
+        load_w(0, 0, HEAD, HEAD0)
         move_scales(0)
-        load_w(tile("head1", [P, PACK, HEAD], F32, HEAD1), 1, 0)
-        load_w(tile("second0", [P, PACK, HEAD], F32), 0, HEAD)
+        load_w(1, 0, HEAD, HEAD1)
+        load_w(0, HEAD, HEAD)
         move_scales(1)
-        load_w(tile("second1", [P, PACK, HEAD], F32, SECOND), 1, HEAD)
-        load_w(tile("third0", [P, PACK, 2 * HEAD], F32), 0, 2 * HEAD)
-        move_scales(2)
-        load_w(tile("third1", [P, PACK, 2 * HEAD], F32), 1, 2 * HEAD)
+        load_w(1, HEAD, HEAD, SECOND1)
+        load_w(0, 2 * HEAD, 2 * HEAD)
+        load_w(1, 2 * HEAD, 2 * HEAD)
 
-        early = {m: tile(f"early{m}", [P, PACK * P], BF16) for m in (0, 1)}
-        late = {m: tile(f"late{m}", [P, PACK * P], BF16) for m in (0, 1)}
-        for m in (0, 1):
-            group(nc.scalar.copy, early[m][:], raws[m, 0])
-        for m in (0, 1):
-            group(nc.scalar.copy, late[m][:], raws[m, 1])
-        gather_words(0)
-        gather_half(1, 0)
-        part(0)
-        for m in (0, 1):
-            quantize(early[m][:], [(m, 0)])
-        gather_half(1, 1, HEAD0)
-        quantize(late[0][:], [(0, 1)])
-        quantize(late[1][:], [(1, 1)])
-        part_halves(1, HEAD1)
-        products((0, 0), (1, 0))
-        for m in (0, 1):
-            products((m, 1))
-            store(m, m + 1, 0, 2)
-
-        second = {m: tile(f"grouped{m}", [P, PASSES, PACK * P], BF16) for m in (2, 3)}
         for a in range(PASSES):
-            for m in (2, 3):
-                group(nc.vector.tensor_copy, second[m][:, a, :], raws[m, a])
+            for m in (0, 1):
+                group(nc.scalar.copy, m, a)
+        gather_whole(0)
+        gather_half(1, 0)
+        part_whole(0)
+        for m in (0, 1):
+            quantize(grouped[m, 0][:], [(m, 0)])
+        gather_half(1, 1, HEAD0)
+        part_half(1, 0, HEAD0 + 4 * N)
+        quantize(grouped[0, 1][:], [(0, 1)])
+        part_half(1, 1)
+        quantize(grouped[1, 1][:], [(1, 1)])
+        gather_half(2, 0, HEAD1 + 2560)
+        gather_half(2, 1, HEAD1)
+        for h in range(2):
+            part_half(2, h)
         for m in (2, 3):
-            quantize_tile(m, second[m])
-        for s in (2, 3):
-            for h in range(2):
-                gather_half(s, h, SECOND + h * SLICE // 2)
-            part_halves(s)
-        for m in (2, 3):
-            products((m, 0))
-            products((m, 1))
-            store(m, m + 1, 0, 2)
-        for s in (2, 3):
-            for m in (0, 2):
+            group_both(m, HEAD1 + 1024 + 2048 * (m - 2))
+        for m, a in ((2, 0), (2, 1), (3, 0)):
+            group_into(nc.vector.tensor_copy, m, a)
+        quantize_both(2)
+        group_into(nc.vector.tensor_copy, 3, 1)
+        quantize_both(3)
+        for h in range(2):
+            gather_half(3, h, SECOND1 + 4 * HALF * h)
+        for h in range(2):
+            part_half(3, h)
+
+        products((0, 0), (1, 0))
+        for s in (1, 2):
+            for m in (0, 1):
                 products((m, s))
-                products((m + 1, s))
-                store(m, m + 2, s, s + 1)
+                if s == 1:
+                    store(m, 0, 2)
+        store_pair(0, 2)
+        for m in (2, 3):
+            for s in range(2):
+                products((m, s))
+            store(m, 0, 2)
+        for m in (2, 3):
+            products((m, 2))
+        store_pair(2, 2)
+        for m in range(4):
+            products((m, 3))
+            if m % 2:
+                store_pair(m - 1, 3)
 
         for m in range(4, M_TILES):
-            grouped = group_tile(m)
-            quantize(grouped[:, 0, :], [(m, 0)])
-            for h in range(2):
-                quantize(grouped[:, 1, :], [(m, 1 + h)], LAST + RAW * (2 * (m - 4) + h))
+            results[m] = tile(f"results{m}", [P, S], F32)
+            group_both(m)
+            for a in range(PASSES):
+                group_into(nc.vector.tensor_copy, m, a)
+            quantize_both(m)
         for m in range(4, M_TILES):
-            for h in range(2):
-                banks = [psum.tile([P, N], F32, name="acc", tag="acc") for j in range(2)]
-                for a in range(PASSES):
-                    for j in range(2):
-                        one_pass(banks[j], m, 2 * h + j, a, a == 0, a * (1 + h))
-                half = tile(f"half{m}{h}", [P, 2 * N], F32, LAST + RAW * (2 * (m - 4) + h))
-                rows = out[P * m : P * (m + 1), 2 * N * h : 2 * N * (h + 1)]
-                if (m, h) != (M_TILES - 1, 1):
-                    for j in range(2):
-                        nc.scalar.activation(half[:, N * j : N * (j + 1)], banks[j][:], GELU, bias=b_cols[:, m : m + 1])
-                    nc.sync.dma_start(out=rows, in_=half[:])
-        for j, c0, c1, queue in ((0, 0, N, nc.sync), (1, 0, N // 2, nc.sync), (1, N // 2, N, nc.scalar)):
-            cols = slice(N * j + c0, N * j + c1)
-            nc.scalar.activation(half[:, cols], banks[j][:, c0:c1], GELU, bias=b_cols[:, m : m + 1])
-            queue.dma_start(out=rows[:, cols], in_=half[:, cols])
+            for s in range(SLICES):
+                if (m, s) != (M_TILES - 1, SLICES - 1):
+                    products((m, s))
+                    if s % 2:
+                        store(m, s - 1, s + 1)
+        store(m, s - 1, s)
+        acc = bank()
+        for a in range(PASSES):
+            one_pass(acc, m, s, a)
+        for h, queue in enumerate((nc.sync, nc.scalar)):
+            cols = slice(N * s + HALF * h, N * s + HALF * (h + 1))
+            nc.scalar.activation(results[m][:, cols], acc[:, HALF * h : HALF * (h + 1)], GELU, bias=b_cols[:, m : m + 1])
+            queue.dma_start(out=out[P * m : P * (m + 1), cols], in_=results[m][:, cols])

@@ -26,10 +26,10 @@ HALF = N // 2
 SLICES = S // N
 ALIGN = 256
 ROWS0 = P - QUAD
-RUNS = ((0, 2), (2, 4))
+RUNS = ((0, 1), (1, 2), (2, 4))
 HEAD = 256
 RAW = 4 * PACK * HEAD
-HEAD0, HEAD1, SECOND1 = 0, RAW, 2 * RAW + 1024
+HEAD0, HEAD1, SECOND1 = 0, RAW, 2 * RAW
 
 
 def tile_list_tab4_gelu_kernel(tc, tab, w, b, offs, out):
@@ -159,9 +159,16 @@ def tile_list_tab4_gelu_kernel(tc, tab, w, b, offs, out):
         def store(m, s0, s1, queue=nc.sync):
             queue.dma_start(out=out[P * m : P * (m + 1), N * s0 : N * s1], in_=results[m][:, N * s0 : N * s1])
 
-        def store_pair(m, s):
+        def store_pair(m, s, queue=nc.sync):
             rows = out[P * m : P * (m + 2), N * s : N * (s + 1)].rearrange("(m p) c -> p m c", p=P)
-            nc.sync.dma_start(out=rows, in_=first[:, m : m + 2, N * s : N * (s + 1)])
+            queue.dma_start(out=rows, in_=first[:, m : m + 2, N * s : N * (s + 1)])
+
+        def store_two(pieces, queue=nc.sync):
+            (m0, s0), (m1, s1) = pieces
+            if m0 == m1:
+                store(m0, s0, s1 + 1, queue)
+            else:
+                store_pair(m0, s0, queue)
 
         def head():
             nc.vector.memset(table_scales[0:ROWS0, :].bitcast(I32), 0)
@@ -192,6 +199,7 @@ def tile_list_tab4_gelu_kernel(tc, tab, w, b, offs, out):
         move_scales(1)
         load_w(1, HEAD, HEAD, SECOND1)
         load_w(0, 2 * HEAD, 2 * HEAD)
+        move_scales(2)
         load_w(1, 2 * HEAD, 2 * HEAD)
 
         for a in range(PASSES):
@@ -203,57 +211,40 @@ def tile_list_tab4_gelu_kernel(tc, tab, w, b, offs, out):
         for m in (0, 1):
             quantize(grouped[m, 0][:], [(m, 0)])
         gather_half(1, 1, HEAD0)
-        part_half(1, 0, HEAD0 + 4 * N)
-        quantize(grouped[0, 1][:], [(0, 1)])
+        for m in (0, 1):
+            quantize(grouped[m, 1][:], [(m, 1)])
+        part_half(1, 0, HEAD1)
         part_half(1, 1)
-        quantize(grouped[1, 1][:], [(1, 1)])
-        gather_half(2, 0, HEAD1 + 2560)
-        gather_half(2, 1, HEAD1)
-        for h in range(2):
-            part_half(2, h)
         for m in (2, 3):
-            group_both(m, HEAD1 + 1024 + 2048 * (m - 2))
-        for m, a in ((2, 0), (2, 1), (3, 0)):
-            group_into(nc.vector.tensor_copy, m, a)
-        quantize_both(2)
-        group_into(nc.vector.tensor_copy, 3, 1)
-        quantize_both(3)
-        for h in range(2):
-            gather_half(3, h, SECOND1 + 4 * HALF * h)
-        for h in range(2):
-            part_half(3, h)
-
-        products((0, 0), (1, 0))
-        for s in (1, 2):
-            for m in (0, 1):
-                products((m, s))
-                if s == 1:
-                    store(m, 0, 2)
-        store_pair(0, 2)
+            group_both(m)
+        for a in range(PASSES):
+            for m in (2, 3):
+                group_into(nc.vector.tensor_copy, m, a)
         for m in (2, 3):
-            for s in range(2):
-                products((m, s))
-            store(m, 0, 2)
-        for m in (2, 3):
-            products((m, 2))
-        store_pair(2, 2)
-        for m in range(4):
-            products((m, 3))
-            if m % 2:
-                store_pair(m - 1, 3)
-
+            quantize_both(m)
+        for s in (2, 3):
+            for h in range(2):
+                gather_half(s, h, SECOND1 + 4 * HALF * h)
+            for h in range(2):
+                part_half(s, h)
         for m in range(4, M_TILES):
             results[m] = tile(f"results{m}", [P, S], F32)
             group_both(m)
             for a in range(PASSES):
                 group_into(nc.vector.tensor_copy, m, a)
             quantize_both(m)
-        for m in range(4, M_TILES):
-            for s in range(SLICES):
-                if (m, s) != (M_TILES - 1, SLICES - 1):
-                    products((m, s))
-                    if s % 2:
-                        store(m, s - 1, s + 1)
+
+        products((0, 0), (1, 0))
+        store_pair(0, 0)
+        twos = [((0, 1), (1, 1)), ((2, 0), (2, 1)), ((3, 0), (3, 1))]
+        twos = twos + [((m, s), (m + 1, s)) for s in (2, 3) for m in (0, 2)]
+        twos = twos + [((m, s), (m, s + 1)) for m in range(4, M_TILES) for s in (0, 2)]
+        for pieces in twos[:-1]:
+            for piece in pieces:
+                products(piece)
+            store_two(pieces)
+        m, s = twos[-1][1]
+        products((m, s - 1))
         store(m, s - 1, s)
         acc = bank()
         for a in range(PASSES):

@@ -26,7 +26,7 @@ HALF = N // 2
 SLICES = S // N
 ALIGN = 256
 ROWS0 = P - QUAD
-RUNS = ((0, 1), (1, 2), (2, 4))
+RUNS = ((0, 2), (2, 4))
 HEAD = 256
 RAW = 4 * PACK * HEAD
 HEAD0, HEAD1, SECOND1 = 0, RAW, 2 * RAW
@@ -196,10 +196,9 @@ def tile_list_tab4_gelu_kernel(tc, tab, w, b, offs, out):
         move_scales(0)
         load_w(1, 0, HEAD, HEAD1)
         load_w(0, HEAD, HEAD)
-        move_scales(1)
         load_w(1, HEAD, HEAD, SECOND1)
         load_w(0, 2 * HEAD, 2 * HEAD)
-        move_scales(2)
+        move_scales(1)
         load_w(1, 2 * HEAD, 2 * HEAD)
 
         for a in range(PASSES):

@@ -23,13 +23,11 @@ PASSES = K // (P * PACK)
 M_TILES = M // P
 N = 512
 HALF = N // 2
-SLICES = S // N
+PAIR = 2 * N
 ALIGN = 256
 ROWS0 = P - QUAD
-RUNS = ((0, 2), (2, 4))
-HEAD = 256
-RAW = 4 * PACK * HEAD
-HEAD0, HEAD1, SECOND1 = 0, RAW, 2 * RAW
+CHUNK = 256
+RAW = 4 * PACK * CHUNK
 
 
 def tile_list_tab4_gelu_kernel(tc, tab, w, b, offs, out):
@@ -47,11 +45,13 @@ def tile_list_tab4_gelu_kernel(tc, tab, w, b, offs, out):
         offsets = keep.tile([P, S // 16], U16, name="offsets", align_bytes=ALIGN)
         words = tile("words", [P, T], I32)
         table_scales = tile("table_scales", [P, T], U8)
-        scales = [tile(f"scales{r}", [P, PASSES * N * (s1 - s0)], U8) for r, (s0, s1) in enumerate(RUNS)]
+        planes = [tile(f"planes{r}", [P, PASSES * PAIR], U8) for r in range(2)]
+        picked_scales = [tile(f"picked_scales{r}", [P, PAIR], U8) for r in range(2)]
         b_rows = tile("b_rows", [P, P], F32)
         b_cols = tile("b_cols", [P, M_TILES], F32)
         identity = tile("identity", [P, P], F32)
-        raws, grouped, codes, code_scales, picked_words, parted, picked_scales = {}, {}, {}, {}, {}, {}, {}
+        results = [tile(f"results{m}", [P, S], F32) for m in range(M_TILES)]
+        raws, grouped, codes, code_scales, picked_words, parted = {}, {}, {}, {}, {}, {}
 
         def load_w(a, c0, width, offset=None):
             raw = tile(f"raw{c0}_{a}", [P, PACK, width], F32, offset)
@@ -60,93 +60,63 @@ def tile_list_tab4_gelu_kernel(tc, tab, w, b, offs, out):
             for j in range(width // P):
                 raws[c0 // P + j, a] = raw[:, :, P * j : P * (j + 1)]
 
-        def gather_scales(r):
-            s0, s1 = RUNS[r]
-            picked_scales[r] = tile(f"picked_scales{r}", [P, N * (s1 - s0)], U8)
-            cols = slice(s0 * N // 16, s1 * N // 16)
-            nc.vector.tensor_copy(picked_scales[r][:], table_scales[:].indirect(offsets[:, cols]))
-
-        def move_scales(r, queue=nc.sync):
+        def move_scales(r):
             for q in (0, 2, 1, 3):
-                queue.dma_start(
-                    out=scales[r][QUAD * q : QUAD * q + 4, :].bitcast(I32),
+                nc.sync.dma_start(
+                    out=planes[r][QUAD * q : QUAD * q + 4, :].bitcast(I32),
                     in_=picked_scales[r][ROWS0 + 8 * q : ROWS0 + 8 * (q + 1), :].bitcast(I32),
                 )
 
-        def group(copy, m, a, offset=None):
-            grouped[m, a] = tile(f"grouped{m}_{a}", [P, PACK * P], BF16, offset)
+        def grouped_tile(m, offset=None):
+            grouped[m] = tile(f"grouped{m}", [P, PASSES, PACK * P], BF16, offset)
+
+        def group(copy, m, a):
             copy(
-                grouped[m, a][:].rearrange("p (c j i) -> p c i j", j=PACK, i=PACK),
+                grouped[m][:, a, :].rearrange("p (c j i) -> p c i j", j=PACK, i=PACK),
                 raws[m, a].rearrange("p i (c j) -> p c i j", j=PACK),
             )
 
-        def group_both(m, offset=None):
-            both = tile(f"both{m}", [P, PASSES, PACK * P], BF16, offset)
-            grouped[m] = both
-            for a in range(PASSES):
-                grouped[m, a] = both[:, a, :]
-
-        def group_into(copy, m, a):
-            copy(
-                grouped[m, a].rearrange("p (c j i) -> p c i j", j=PACK, i=PACK),
-                raws[m, a].rearrange("p i (c j) -> p c i j", j=PACK),
-            )
-
-        def quantize(src, pieces, offset=None):
-            m, a = pieces[0]
-            piece_codes = tile(f"codes{m}_{a}", [P, P * len(pieces)], U32, offset)
-            piece_scales = tile(f"code_scales{m}_{a}", [P, P * len(pieces)], U8)
+        def quantize(m, a0, a1):
+            width = P * (a1 - a0)
+            piece_codes = tile(f"codes{m}_{a0}", [P, width], U32)
+            piece_scales = tile(f"code_scales{m}_{a0}", [P, width], U8)
+            src = grouped[m][:, a0:a1, :].rearrange("p a c -> p (a c)")
             nc.vector.quantize_mx(out=piece_codes[:].bitcast(E4M3), scales=piece_scales[:], in_=src)
-            for j, piece in enumerate(pieces):
-                codes[piece] = piece_codes[:, P * j : P * (j + 1)]
-                code_scales[piece] = piece_scales[:, P * j : P * (j + 1)]
+            for a in range(a0, a1):
+                codes[m, a] = piece_codes[:, P * (a - a0) : P * (a - a0 + 1)]
+                code_scales[m, a] = piece_scales[:, P * (a - a0) : P * (a - a0 + 1)]
 
-        def quantize_both(m):
-            quantize(grouped[m][:].rearrange("p a c -> p (a c)"), [(m, a) for a in range(PASSES)])
+        def gather(s, j0, width, offset=None):
+            picked_words[s, j0] = tile(f"picked_words{s}_{j0}", [P, width], I32, offset)
+            cols = slice((N * s + j0) // 16, (N * s + j0 + width) // 16)
+            nc.vector.tensor_copy(picked_words[s, j0][:].bitcast(U32), words[:].bitcast(U32).indirect(offsets[:, cols]))
 
-        def gather_half(s, h, offset=None):
-            picked_words[s, h] = tile(f"picked_words{s}_{h}", [P, HALF], I32, offset)
-            cols = slice((2 * s + h) * HALF // 16, (2 * s + h + 1) * HALF // 16)
-            nc.vector.tensor_copy(picked_words[s, h][:].bitcast(U32), words[:].bitcast(U32).indirect(offsets[:, cols]))
-
-        def part_half(s, h, offset=None):
+        def part(s, j0, width, offset=None):
             if s not in parted:
                 parted[s] = tile(f"parted{s}", [P, PASSES, 2 * N], U8, offset)
             nc.vector.tensor_copy(
-                parted[s][:, :, N * h : N * (h + 1)].bitcast(U16),
-                picked_words[s, h][:].bitcast(U16).rearrange("p (n a) -> p a n", a=PASSES),
-            )
-
-        def gather_whole(s, offset=None):
-            picked_words[s] = tile(f"picked_words{s}", [P, N], I32, offset)
-            cols = slice(s * N // 16, (s + 1) * N // 16)
-            nc.vector.tensor_copy(picked_words[s][:].bitcast(U32), words[:].bitcast(U32).indirect(offsets[:, cols]))
-
-        def part_whole(s, offset=None):
-            parted[s] = tile(f"parted{s}", [P, PASSES, 2 * N], U8, offset)
-            halves = parted[s][:].rearrange("p a c -> p (a c)").bitcast(U16)
-            nc.vector.tensor_copy(
-                halves.rearrange("p (a n) -> p a n", a=PASSES),
-                picked_words[s][:].bitcast(U16).rearrange("p (n a) -> p a n", a=PASSES),
-            )
-
-        def one_pass(acc, m, s, a, piece=None):
-            piece = a if piece is None else piece
-            r = [s0 <= s < s1 for s0, s1 in RUNS].index(True)
-            s0, s1 = RUNS[r]
-            j0 = N * ((s1 - s0) * a + s - s0)
-            nc.tensor.matmul_mx(
-                out=acc[:],
-                lhsT=codes[m, piece].bitcast(E4M3),
-                lhsT_scale=code_scales[m, piece],
-                rhs=parted[s][:, a, :].bitcast(E2M1),
-                rhs_scale=scales[r][:, j0 : j0 + N],
-                start=a == 0,
-                stop=a == PASSES - 1,
+                parted[s][:, :, 2 * j0 : 2 * (j0 + width)].bitcast(U16),
+                picked_words[s, j0][:].bitcast(U16).rearrange("p (n a) -> p a n", a=PASSES),
             )
 
         def bank():
             return psum.tile([P, N], F32, name="acc", tag="acc")
+
+        def one_pass(acc, m, s, a):
+            j0 = PAIR * a + N * (s % 2)
+            nc.tensor.matmul_mx(
+                out=acc[:],
+                lhsT=codes[m, a].bitcast(E4M3),
+                lhsT_scale=code_scales[m, a],
+                rhs=parted[s][:, a, :].bitcast(E2M1),
+                rhs_scale=planes[s // 2][:, j0 : j0 + N],
+                start=a == 0,
+                stop=a == PASSES - 1,
+            )
+
+        def finish(acc, m, s, c0=0, c1=N):
+            cols = slice(N * s + c0, N * s + c1)
+            nc.scalar.activation(results[m][:, cols], acc[:, c0:c1], GELU, bias=b_cols[:, m : m + 1])
 
         def products(*pieces):
             banks = [bank() for piece in pieces]
@@ -154,101 +124,91 @@ def tile_list_tab4_gelu_kernel(tc, tab, w, b, offs, out):
                 for (m, s), acc in zip(pieces, banks):
                     one_pass(acc, m, s, a)
             for (m, s), acc in zip(pieces, banks):
-                nc.scalar.activation(results[m][:, N * s : N * (s + 1)], acc[:], GELU, bias=b_cols[:, m : m + 1])
+                finish(acc, m, s)
 
-        def store(m, s0, s1, queue=nc.sync):
-            queue.dma_start(out=out[P * m : P * (m + 1), N * s0 : N * s1], in_=results[m][:, N * s0 : N * s1])
+        def store(m, c0, c1, queue=nc.sync):
+            queue.dma_start(out=out[P * m : P * (m + 1), c0:c1], in_=results[m][:, c0:c1])
 
-        def store_pair(m, s, queue=nc.sync):
-            rows = out[P * m : P * (m + 2), N * s : N * (s + 1)].rearrange("(m p) c -> p m c", p=P)
-            queue.dma_start(out=rows, in_=first[:, m : m + 2, N * s : N * (s + 1)])
+        nc.vector.memset(table_scales[0:ROWS0, :].bitcast(I32), 0)
+        nc.sync.dma_start(offsets[:], offs)
+        nc.sync.dma_start(
+            out=table_scales[ROWS0:P, :].bitcast(I32),
+            in_=tab[0, 4 * P * T :].rearrange("(a g t) -> g a t", a=PASSES, t=T).bitcast(I32),
+        )
+        nc.sync.dma_start(out=words[:], in_=tab[0, 0 : 4 * P * T].rearrange("(p c) -> p c", p=P).bitcast(I32))
+        nc.scalar.dma_start(out=b_rows[P - M_TILES : P, :], in_=b.rearrange("(m p) -> m p", p=P))
+        make_identity(nc, identity[:])
+        nc.scalar.activation(b_rows[0 : P - M_TILES, :], identity[0 : P - M_TILES, :], GELU, scale=0.0)
+        for r in range(2):
+            nc.gpsimd.memset(planes[r][:].bitcast(I32), 0)
+        b_bank = bank()
+        nc.tensor.transpose(b_bank[:, 0:P], b_rows[:], identity[:])
+        nc.scalar.copy(b_cols[:], b_bank[:, P - M_TILES : P])
+        for r in range(2):
+            cols = slice(r * PAIR // 16, (r + 1) * PAIR // 16)
+            nc.vector.tensor_copy(picked_scales[r][:], table_scales[:].indirect(offsets[:, cols]))
 
-        def store_two(pieces, queue=nc.sync):
-            (m0, s0), (m1, s1) = pieces
-            if m0 == m1:
-                store(m0, s0, s1 + 1, queue)
-            else:
-                store_pair(m0, s0, queue)
-
-        def head():
-            nc.vector.memset(table_scales[0:ROWS0, :].bitcast(I32), 0)
-            nc.sync.dma_start(offsets[:], offs)
-            nc.sync.dma_start(
-                out=table_scales[ROWS0:P, :].bitcast(I32),
-                in_=tab[0, 4 * P * T :].rearrange("(a g t) -> g a t", a=PASSES, t=T).bitcast(I32),
-            )
-            nc.sync.dma_start(out=words[:], in_=tab[0, 0 : 4 * P * T].rearrange("(p c) -> p c", p=P).bitcast(I32))
-            nc.scalar.dma_start(out=b_rows[P - M_TILES : P, :], in_=b.rearrange("(m p) -> m p", p=P))
-            make_identity(nc, identity[:])
-            nc.scalar.activation(b_rows[0 : P - M_TILES, :], identity[0 : P - M_TILES, :], GELU, scale=0.0)
-            for r in range(len(RUNS)):
-                nc.gpsimd.memset(scales[r][:].bitcast(I32), 0)
-            b_bank = bank()
-            nc.tensor.transpose(b_bank[:, 0:P], b_rows[:], identity[:])
-            nc.scalar.copy(b_cols[:], b_bank[:, P - M_TILES : P])
-            for r in range(len(RUNS)):
-                gather_scales(r)
-
-        first = tile("first", [P, 4, S], F32)
-        results = {m: first[:, m, :] for m in range(4)}
-        head()
-        load_w(0, 0, HEAD, HEAD0)
+        load_w(0, 0, CHUNK, 0)
         move_scales(0)
-        load_w(1, 0, HEAD, HEAD1)
-        load_w(0, HEAD, HEAD)
-        load_w(1, HEAD, HEAD, SECOND1)
-        load_w(0, 2 * HEAD, 2 * HEAD)
+        load_w(1, 0, CHUNK, RAW)
+        load_w(0, CHUNK, CHUNK)
+        load_w(1, CHUNK, CHUNK, 2 * RAW)
+        load_w(0, 2 * CHUNK, 2 * CHUNK)
+        load_w(1, 2 * CHUNK, CHUNK, 3 * RAW)
+        load_w(1, 3 * CHUNK, CHUNK, 4 * RAW)
         move_scales(1)
-        load_w(1, 2 * HEAD, 2 * HEAD)
 
+        for m in (0, 1):
+            grouped_tile(m)
         for a in range(PASSES):
             for m in (0, 1):
                 group(nc.scalar.copy, m, a)
-        gather_whole(0)
-        gather_half(1, 0)
-        part_whole(0)
+        gather(0, 0, N)
+        gather(1, 0, HALF)
+        part(0, 0, N)
         for m in (0, 1):
-            quantize(grouped[m, 0][:], [(m, 0)])
-        gather_half(1, 1, HEAD0)
+            quantize(m, 0, 1)
+        gather(1, HALF, HALF, 0)
         for m in (0, 1):
-            quantize(grouped[m, 1][:], [(m, 1)])
-        part_half(1, 0, HEAD1)
-        part_half(1, 1)
-        for m in (2, 3):
-            group_both(m)
-        for a in range(PASSES):
-            for m in (2, 3):
-                group_into(nc.vector.tensor_copy, m, a)
-        for m in (2, 3):
-            quantize_both(m)
-        for s in (2, 3):
-            for h in range(2):
-                gather_half(s, h, SECOND1 + 4 * HALF * h)
-            for h in range(2):
-                part_half(s, h)
-        for m in range(4, M_TILES):
-            results[m] = tile(f"results{m}", [P, S], F32)
-            group_both(m)
+            quantize(m, 1, 2)
+        part(1, 0, HALF, RAW)
+        part(1, HALF, HALF)
+
+        def prepare(pair, offset=None):
+            for j, m in enumerate(pair):
+                grouped_tile(m, None if offset is None else offset + j * RAW // 2)
             for a in range(PASSES):
-                group_into(nc.vector.tensor_copy, m, a)
-            quantize_both(m)
+                for m in pair:
+                    group(nc.vector.tensor_copy, m, a)
+            for m in pair:
+                quantize(m, 0, PASSES)
+
+        prepare((2, 3))
+        gather(2, 0, N, 2 * RAW)
+        prepare((4, 5))
+        prepare((6, 7), 3 * RAW)
+        gather(3, 0, N, 4 * RAW)
+        part(2, 0, N, 4 * RAW + RAW // 2)
+        part(3, 0, N)
 
         products((0, 0), (1, 0))
-        store_pair(0, 0)
-        twos = [((0, 1), (1, 1)), ((2, 0), (2, 1)), ((3, 0), (3, 1))]
-        twos = twos + [((m, s), (m + 1, s)) for s in (2, 3) for m in (0, 2)]
-        twos = twos + [((m, s), (m, s + 1)) for m in range(4, M_TILES) for s in (0, 2)]
-        for pieces in twos[:-1]:
-            for piece in pieces:
-                products(piece)
-            store_two(pieces)
-        m, s = twos[-1][1]
-        products((m, s - 1))
-        store(m, s - 1, s)
+        for m in (0, 1):
+            products((m, 1))
+            store(m, 0, PAIR)
+        for m in range(2, M_TILES):
+            for s in (0, 1):
+                products((m, s))
+            store(m, 0, PAIR)
+        for m in range(M_TILES - 1):
+            for s in (2, 3):
+                products((m, s))
+            store(m, PAIR, S)
+        m = M_TILES - 1
+        products((m, 2))
+        store(m, PAIR, PAIR + N)
         acc = bank()
         for a in range(PASSES):
-            one_pass(acc, m, s, a)
+            one_pass(acc, m, 3, a)
         for h, queue in enumerate((nc.sync, nc.scalar)):
-            cols = slice(N * s + HALF * h, N * s + HALF * (h + 1))
-            nc.scalar.activation(results[m][:, cols], acc[:, HALF * h : HALF * (h + 1)], GELU, bias=b_cols[:, m : m + 1])
-            queue.dma_start(out=out[P * m : P * (m + 1), cols], in_=results[m][:, cols])
+            finish(acc, m, 3, HALF * h, HALF * (h + 1))
+            store(m, 3 * N + HALF * h, 3 * N + HALF * (h + 1), queue)

@@ -50,7 +50,8 @@ def tile_list_tab4_gelu_kernel(tc, tab, w, b, offs, out):
         b_rows = tile("b_rows", [P, P], F32)
         b_cols = tile("b_cols", [P, M_TILES], F32)
         identity = tile("identity", [P, P], F32)
-        results = [tile(f"results{m}", [P, S], F32) for m in range(M_TILES)]
+        first = tile("first", [P, 2, S], F32)
+        results = [first[:, m, :] for m in range(2)] + [tile(f"results{m}", [P, S], F32) for m in range(2, M_TILES)]
         raws, grouped, codes, code_scales, picked_words, parted = {}, {}, {}, {}, {}, {}
 
         def load_w(a, c0, width, offset=None):
@@ -152,10 +153,11 @@ def tile_list_tab4_gelu_kernel(tc, tab, w, b, offs, out):
         move_scales(0)
         load_w(1, 0, CHUNK, RAW)
         load_w(0, CHUNK, CHUNK)
-        load_w(1, CHUNK, CHUNK, 2 * RAW)
-        load_w(0, 2 * CHUNK, 2 * CHUNK)
-        load_w(1, 2 * CHUNK, CHUNK, 3 * RAW)
-        load_w(1, 3 * CHUNK, CHUNK, 4 * RAW)
+        load_w(1, CHUNK, CHUNK)
+        load_w(0, 2 * CHUNK, CHUNK)
+        load_w(1, 2 * CHUNK, CHUNK, 2 * RAW)
+        load_w(0, 3 * CHUNK, CHUNK)
+        load_w(1, 3 * CHUNK, CHUNK, 3 * RAW)
         move_scales(1)
 
         for m in (0, 1):
@@ -184,11 +186,11 @@ def tile_list_tab4_gelu_kernel(tc, tab, w, b, offs, out):
                 quantize(m, 0, PASSES)
 
         prepare((2, 3))
-        gather(2, 0, N, 2 * RAW)
         prepare((4, 5))
-        prepare((6, 7), 3 * RAW)
-        gather(3, 0, N, 4 * RAW)
-        part(2, 0, N, 4 * RAW + RAW // 2)
+        gather(2, 0, N, 2 * RAW)
+        prepare((6, 7))
+        part(2, 0, N, 3 * RAW + RAW // 2)
+        gather(3, 0, N, 3 * RAW)
         part(3, 0, N)
 
         products((0, 0), (1, 0))
@@ -199,7 +201,12 @@ def tile_list_tab4_gelu_kernel(tc, tab, w, b, offs, out):
             for s in (0, 1):
                 products((m, s))
             store(m, 0, PAIR)
-        for m in range(M_TILES - 1):
+        for s in (2, 3):
+            for m in (0, 1):
+                products((m, s))
+            rows = out[0 : 2 * P, N * s : N * (s + 1)].rearrange("(m p) c -> p m c", p=P)
+            nc.sync.dma_start(out=rows, in_=first[:, :, N * s : N * (s + 1)])
+        for m in range(2, M_TILES - 1):
             for s in (2, 3):
                 products((m, s))
             store(m, PAIR, S)

@@ -103,14 +103,14 @@ def tile_list_tab4_gelu_kernel(tc, tab, w, b, offs, out):
         def bank():
             return psum.tile([P, N], F32, name="acc", tag="acc")
 
-        def one_pass(acc, m, s, a):
+        def one_pass(acc, m, s, a, c0=0, c1=N):
             j0 = PAIR * a + N * (s % 2)
             nc.tensor.matmul_mx(
-                out=acc[:],
+                out=acc[:, c0:c1],
                 lhsT=codes[m, a].bitcast(E4M3),
                 lhsT_scale=code_scales[m, a],
-                rhs=parted[s][:, a, :].bitcast(E2M1),
-                rhs_scale=planes[s // 2][:, j0 : j0 + N],
+                rhs=parted[s][:, a, 2 * c0 : 2 * c1].bitcast(E2M1),
+                rhs_scale=planes[s // 2][:, j0 + c0 : j0 + c1],
                 start=a == 0,
                 stop=a == PASSES - 1,
             )
@@ -194,9 +194,14 @@ def tile_list_tab4_gelu_kernel(tc, tab, w, b, offs, out):
         part(3, 0, N)
 
         products((0, 0), (1, 0))
-        for m in (0, 1):
-            products((m, 1))
-            store(m, 0, PAIR)
+        acc = bank()
+        for h in range(2):
+            for a in range(PASSES):
+                one_pass(acc, 0, 1, a, HALF * h, HALF * (h + 1))
+        finish(acc, 0, 1)
+        store(0, 0, PAIR)
+        products((1, 1))
+        store(1, 0, PAIR)
         for m in range(2, M_TILES):
             for s in (0, 1):
                 products((m, s))

from contextlib import ExitStack

import concourse.mybir as mybir
from concourse.masks import make_identity

K, M, T, S = 1024, 1024, 4096, 2048
FLOPS = 2 * K * M * S

F32 = mybir.dt.float32
BF16 = mybir.dt.bfloat16
I32 = mybir.dt.int32
U32 = mybir.dt.uint32
U16 = mybir.dt.uint16
U8 = mybir.dt.uint8
E4M3 = mybir.dt.float8_e4m3fn_x4
E2M1 = mybir.dt.float4_e2m1fn_x4
GELU = mybir.ActivationFunctionType.Gelu_apprx_tanh

P = 128
QUAD = 32
PACK = 4
PASSES = K // (P * PACK)
M_TILES = M // P
N = 512
HALF = N // 2
PAIR = 2 * N
ALIGN = 256
ROWS0 = P - QUAD
CHUNK = 256
RAW = 4 * PACK * CHUNK


def tile_list_tab4_gelu_kernel(tc, tab, w, b, offs, out):
    nc = tc.nc
    with ExitStack() as ctx:
        keep = ctx.enter_context(tc.tile_pool(name="keep", bufs=1))
        shared = ctx.enter_context(tc.tile_pool(name="shared", bufs=1))
        psum = ctx.enter_context(tc.psum_pool(name="psum", bufs=8))

        def tile(name, shape, dtype, offset=None):
            if offset is None:
                return keep.tile(shape, dtype, name=name, align_bytes=ALIGN)
            return shared.tile(shape, dtype, name=name, offset=offset, align_bytes=ALIGN)

        offsets = keep.tile([P, S // 16], U16, name="offsets", align_bytes=ALIGN)
        words = tile("words", [P, T], I32)
        table_scales = tile("table_scales", [P, T], U8)
        planes = [tile(f"planes{r}", [P, PASSES * PAIR], U8) for r in range(2)]
        picked_scales = [tile(f"picked_scales{r}", [P, PAIR], U8) for r in range(2)]
        b_rows = tile("b_rows", [P, P], F32)
        b_cols = tile("b_cols", [P, M_TILES], F32)
        identity = tile("identity", [P, P], F32)
        first = tile("first", [P, 2, S], F32)
        results = [first[:, m, :] for m in range(2)] + [tile(f"results{m}", [P, S], F32) for m in range(2, M_TILES)]
        raws, grouped, codes, code_scales, picked_words, parted = {}, {}, {}, {}, {}, {}

        def load_w(a, c0, width, offset=None):
            raw = tile(f"raw{c0}_{a}", [P, PACK, width], F32, offset)
            rows = w[P * PACK * a : P * PACK * (a + 1), c0 : c0 + width].rearrange("(p i) c -> p i c", i=PACK)
            nc.sync.dma_start(out=raw[:], in_=rows)
            for j in range(width // P):
                raws[c0 // P + j, a] = raw[:, :, P * j : P * (j + 1)]

        def move_scales(r):
            for q in (0, 2, 1, 3):
                nc.sync.dma_start(
                    out=planes[r][QUAD * q : QUAD * q + 4, :].bitcast(I32),
                    in_=picked_scales[r][ROWS0 + 8 * q : ROWS0 + 8 * (q + 1), :].bitcast(I32),
                )

        def grouped_tile(m, offset=None):
            grouped[m] = tile(f"grouped{m}", [P, PASSES, PACK * P], BF16, offset)

        def group(copy, m, a):
            copy(
                grouped[m][:, a, :].rearrange("p (c j i) -> p c i j", j=PACK, i=PACK),
                raws[m, a].rearrange("p i (c j) -> p c i j", j=PACK),
            )

        def quantize(m, a0, a1):
            width = P * (a1 - a0)
            piece_codes = tile(f"codes{m}_{a0}", [P, width], U32)
            piece_scales = tile(f"code_scales{m}_{a0}", [P, width], U8)
            src = grouped[m][:, a0:a1, :].rearrange("p a c -> p (a c)")
            nc.vector.quantize_mx(out=piece_codes[:].bitcast(E4M3), scales=piece_scales[:], in_=src)
            for a in range(a0, a1):
                codes[m, a] = piece_codes[:, P * (a - a0) : P * (a - a0 + 1)]
                code_scales[m, a] = piece_scales[:, P * (a - a0) : P * (a - a0 + 1)]

        def gather(s, j0, width, offset=None):
            picked_words[s, j0] = tile(f"picked_words{s}_{j0}", [P, width], I32, offset)
            cols = slice((N * s + j0) // 16, (N * s + j0 + width) // 16)
            nc.vector.tensor_copy(picked_words[s, j0][:].bitcast(U32), words[:].bitcast(U32).indirect(offsets[:, cols]))

        def part(s, j0, width, offset=None):
            if s not in parted:
                parted[s] = tile(f"parted{s}", [P, PASSES, 2 * N], U8, offset)
            nc.vector.tensor_copy(
                parted[s][:, :, 2 * j0 : 2 * (j0 + width)].bitcast(U16),
                picked_words[s, j0][:].bitcast(U16).rearrange("p (n a) -> p a n", a=PASSES),
            )

        def bank():
            return psum.tile([P, N], F32, name="acc", tag="acc")

        def one_pass(acc, m, s, a, c0=0, c1=N):
            j0 = PAIR * a + N * (s % 2)
            nc.tensor.matmul_mx(
                out=acc[:, c0:c1],
                lhsT=codes[m, a].bitcast(E4M3),
                lhsT_scale=code_scales[m, a],
                rhs=parted[s][:, a, 2 * c0 : 2 * c1].bitcast(E2M1),
                rhs_scale=planes[s // 2][:, j0 + c0 : j0 + c1],
                start=a == 0,
                stop=a == PASSES - 1,
            )

        def finish(acc, m, s, c0=0, c1=N):
            cols = slice(N * s + c0, N * s + c1)
            nc.scalar.activation(results[m][:, cols], acc[:, c0:c1], GELU, bias=b_cols[:, m : m + 1])

        def products(*pieces):
            banks = [bank() for piece in pieces]
            for a in range(PASSES):
                for (m, s), acc in zip(pieces, banks):
                    one_pass(acc, m, s, a)
            for (m, s), acc in zip(pieces, banks):
                finish(acc, m, s)

        def store(m, c0, c1, queue=nc.sync):
            queue.dma_start(out=out[P * m : P * (m + 1), c0:c1], in_=results[m][:, c0:c1])

        nc.vector.memset(table_scales[0:ROWS0, :].bitcast(I32), 0)
        nc.sync.dma_start(offsets[:], offs)
        nc.sync.dma_start(
            out=table_scales[ROWS0:P, :].bitcast(I32),
            in_=tab[0, 4 * P * T :].rearrange("(a g t) -> g a t", a=PASSES, t=T).bitcast(I32),
        )
        nc.sync.dma_start(out=words[:], in_=tab[0, 0 : 4 * P * T].rearrange("(p c) -> p c", p=P).bitcast(I32))
        nc.scalar.dma_start(out=b_rows[P - M_TILES : P, :], in_=b.rearrange("(m p) -> m p", p=P))
        make_identity(nc, identity[:])
        nc.scalar.activation(b_rows[0 : P - M_TILES, :], identity[0 : P - M_TILES, :], GELU, scale=0.0)
        for r in range(2):
            nc.gpsimd.memset(planes[r][:].bitcast(I32), 0)
        b_bank = bank()
        nc.tensor.transpose(b_bank[:, 0:P], b_rows[:], identity[:])
        nc.scalar.copy(b_cols[:], b_bank[:, P - M_TILES : P])
        for r in range(2):
            cols = slice(r * PAIR // 16, (r + 1) * PAIR // 16)
            nc.vector.tensor_copy(picked_scales[r][:], table_scales[:].indirect(offsets[:, cols]))

        load_w(0, 0, CHUNK, 0)
        move_scales(0)
        load_w(1, 0, CHUNK, RAW)
        load_w(0, CHUNK, CHUNK)
        load_w(1, CHUNK, CHUNK)
        load_w(0, 2 * CHUNK, CHUNK)
        load_w(1, 2 * CHUNK, CHUNK, 2 * RAW)
        load_w(0, 3 * CHUNK, CHUNK)
        load_w(1, 3 * CHUNK, CHUNK, 3 * RAW)
        move_scales(1)

        for m in (0, 1):
            grouped_tile(m)
        for a in range(PASSES):
            for m in (0, 1):
                group(nc.scalar.copy, m, a)
        gather(0, 0, N)
        gather(1, 0, HALF)
        part(0, 0, N)
        for m in (0, 1):
            quantize(m, 0, 1)
        gather(1, HALF, HALF, 0)
        for m in (0, 1):
            quantize(m, 1, 2)
        part(1, 0, HALF, RAW)
        part(1, HALF, HALF)

        def prepare(pair, offset=None):
            for j, m in enumerate(pair):
                grouped_tile(m, None if offset is None else offset + j * RAW // 2)
            for a in range(PASSES):
                for m in pair:
                    group(nc.vector.tensor_copy, m, a)
            for m in pair:
                quantize(m, 0, PASSES)

        prepare((2, 3))
        prepare((4, 5))
        gather(2, 0, N, 2 * RAW)
        prepare((6, 7))
        part(2, 0, N, 3 * RAW + RAW // 2)
        gather(3, 0, N, 3 * RAW)
        part(3, 0, N)

        products((0, 0), (1, 0))
        acc = bank()
        for h in range(2):
            for a in range(PASSES):
                one_pass(acc, 0, 1, a, HALF * h, HALF * (h + 1))
        finish(acc, 0, 1)
        store(0, 0, PAIR)
        products((1, 1))
        store(1, 0, PAIR)
        for m in range(2, M_TILES):
            for s in (0, 1):
                products((m, s))
            store(m, 0, PAIR)
        for s in (2, 3):
            for m in (0, 1):
                products((m, s))
            rows = out[0 : 2 * P, N * s : N * (s + 1)].rearrange("(m p) c -> p m c", p=P)
            nc.sync.dma_start(out=rows, in_=first[:, :, N * s : N * (s + 1)])
        for m in range(2, M_TILES - 1):
            for s in (2, 3):
                products((m, s))
            store(m, PAIR, S)
        m = M_TILES - 1
        products((m, 2))
        store(m, PAIR, PAIR + N)
        acc = bank()
        for a in range(PASSES):
            one_pass(acc, m, 3, a)
        for h, queue in enumerate((nc.sync, nc.scalar)):
            finish(acc, m, 3, HALF * h, HALF * (h + 1))
            store(m, 3 * N + HALF * h, 3 * N + HALF * (h + 1), queue)
